import numpy as np, ml_dtypes
CORES = [36,164,52,180,100,228,116,244]
N = 8
import mx_ref
BF = ml_dtypes.bfloat16
def pick(q, e):
    c = np.concatenate([q[0].reshape(128, -1, 4), np.zeros((128, 1, 4), np.uint8)], axis=1); s = np.concatenate([q[1], np.ones((16, 1), np.uint8)], axis=1)
    return (np.ascontiguousarray(c[:, e].reshape(128, -1)), np.ascontiguousarray(s[:, e]))
def join(*qs):
    return (np.concatenate([q[0] for q in qs], axis=1), np.concatenate([q[1] for q in qs], axis=1))
def put(q, e, v):
    c, s = q[0].reshape(128, -1, 4).copy(), q[1].copy(); c[:, e] = v[0].reshape(128, -1, 4); s[:, e] = v[1]
    return (c.reshape(128, -1), s)
def pk(c, s):
    return (np.ascontiguousarray(c), mx_ref.live(s))
def emit(q):
    return q[0], q[1]
def decode(q):
    o = []
    for b in range(4):
        e = np.zeros((128, 128, 4), np.float32); e[np.arange(128), np.arange(128), b] = 1
        o.append(mx_ref.matmul(mx_ref.quantize(e.reshape(128, 512).astype(BF)), q))
    return np.stack(o, axis=2).reshape(128, -1)
def cut(t, i, w=512):
    return t[:, w * i:w * i + w]
def f(rng, *shape):
    return mx_ref.flush((rng.standard_normal(shape, dtype=np.float32) * np.exp2(rng.integers(-2, 3, shape[:-1] + (1,)))).astype(BF))
def wide(rng, *shape, cols=0):
    v = rng.standard_normal(shape, dtype=np.float32) * np.exp2(rng.integers(-12, 13, shape)).astype(np.float32)
    if cols: v *= np.repeat(np.exp2(rng.integers(-cols, cols + 1, shape[:-2] + (1, shape[-1] // 4))) * (rng.random(shape[:-2] + (1, shape[-1] // 4)) > 0.0625), 4, axis=-1).astype(np.float32)
    return mx_ref.flush(v.astype(BF))
P, K, R, O = 192, 32, 3, 1
def big(v):
    v = v.astype(np.float32)
    v[np.abs(v) < np.float32(2.0 ** -16)] = 0
    return v.astype(BF)
def plain(rng):
    u = np.array(f(rng, N, 128, 512))
    u[:, :, 4 * R:] = 0
    return {"c": big(f(rng, N, 128, 4 * P)), "u": u, "w": f(rng, N, 128, 512 * O)}
def bf(v, *shape):
    return np.ascontiguousarray(v).reshape(shape).astype(np.float32).astype(BF)
def signs(rng):
    return rng.choice([-1.0, 1.0], (128, 1, 4))
def heavy(rng, way):
    d, g = plain(rng), signs(rng)
    size = np.exp2(rng.integers(0, 3, (N, P)))
    size[np.arange(N), rng.integers(0, P, N)] = 1024
    d["c"] = bf((1 + rng.random((N, 128, P, 4))) * size[:, None, :, None] * g * 2.0 ** 18, N, 128, 4 * P)
    d["u"][:, :, :4 * R] = bf((1 + rng.random((N, 128, R, 4))) * g * np.asarray(way)[:, None] * 2.0 ** 28, N, 128, 4 * R)
    return d
def setup_inputs(rng):
    return plain(rng)
def setup_inputs_one(rng):
    return heavy(rng, np.ones(R))
def setup_inputs_chain(rng):
    return heavy(rng, np.where(np.arange(R) == 0, 1.0, -1.0))
def setup_inputs_apart(rng):
    d, g = plain(rng), signs(rng)
    v = np.zeros((N, 128, P, 4))
    for r in range(N):
        at = rng.permutation(P)
        a, b = at[:K], at[K:2 * K]
        v[r][np.arange(K), a] = 32 * (1 + rng.random((K, 4)))
        v[r][np.arange(K), b] = 32 * (1 + rng.random((K, 4)))
        v[r][64:96, a] = -(1 + 0.125 * rng.random((32, K, 4)))
        v[r][64:96, at[K:]] = 4096
        v[r][96:, at[K:]] = 1 + rng.random((32, P - K, 4))
    d["c"] = bf(v * g * 2.0 ** 18, N, 128, 4 * P)
    q = (1 + rng.random((N, 128, R, 4))) * g
    q[:, :64] = 0
    d["u"][:, :, :4 * R] = bf(q, N, 128, 4 * R)
    return d
def setup_inputs_ties(rng):
    d, g = plain(rng), signs(rng)
    v = np.abs(d["c"].astype(np.float32)).reshape(N, 128, P, 4)[:, :, :8] * g
    v[:, :, 0] = 0
    h = [rng.permutation(np.arange(P) % 8) for r in range(N)]
    for r in range(0, N, 2):
        i = int(np.flatnonzero(h[r] == 0)[0])
        h[r][i] = h[r][0]
        h[r][0] = 0
    d["c"] = bf(np.stack([v[r][:, h[r]] for r in range(N)]), N, 128, 4 * P)
    d["u"][:, :, :4] = bf(np.abs(d["u"][:, :, :4].astype(np.float32)).reshape(N, 128, 1, 4) * g, N, 128, 4)
    return d
def setup_inputs_spread(rng):
    d = plain(rng)
    d["u"][:, :, 4:8] = 0
    return {**d, "c": big(wide(rng, N, 128, 4 * P, cols=6))}
def check_inputs(d):
    b = []
    for k, low in (("c", 2.0 ** -16), ("u", 2.0 ** -30), ("w", 2.0 ** -30)):
        v = np.abs(d[k].astype(np.float32))
        if not (np.isfinite(v).all() and ((v == 0) | (v >= low) & (v <= 2.0 ** 30)).all()): b.append("a value of " + k)
    if (d["u"][:, :, 4 * R:].astype(np.float32) != 0).any(): b.append("u has numbers behind its first R columns")
    return b
def reference(c, u, w):
    tg = np.zeros((N, R, K), np.float32)
    cs = [mx_ref.quantize(np.ascontiguousarray(c[r])) for r in range(N)]
    qu = [mx_ref.quantize(np.ascontiguousarray(u[r])) for r in range(N)]
    half, zero = np.float32(0.5), np.float32(0)
    for t in range(R):
        left, sent = [], []
        for r in range(N):
            s = mx_ref.matmul(qu[r], cs[r])[t] + zero
            left.append(np.argsort(s, kind="stable")[:K])
            sent.append(pick(cs[r], left[r]))
        for r in range(N):
            a = sent[r ^ (1 << t)]
            z = mx_ref.matmul(pick(a, np.concatenate([np.arange(K), np.full(128 - K, -1)])), cs[r])[:K] + zero
            z[:, left[r]] = -np.inf
            to = np.argmax(z, axis=1)
            merge = np.sort(np.unique(to, return_index=True)[1])
            fill = np.setdiff1d(np.arange(K), merge)
            places = np.sort(left[r])[:len(fill)]
            v = decode(join(cs[r], a)).reshape(128, P + K, 4)
            v[:, to[merge]] = half * v[:, to[merge]] + half * v[:, P + merge]
            new = mx_ref.quantize(np.ascontiguousarray(v[:, :P]).reshape(128, -1).astype(BF))
            q = put(cs[r], to[merge], pick(new, to[merge]))
            cs[r] = put(q, places, pick(a, fill))
            tg[r, t, merge] = to[merge]
            tg[r, t, fill] = -1 - places
    oc, osc, y = np.zeros((N, 128, 4 * P), np.uint8), np.zeros((N, 16, P), np.uint8), np.zeros((N, 128, O * P), np.float32)
    for r in range(N):
        oc[r], osc[r] = emit(cs[r])
        for o in range(O):
            y[r, :, o * P:o * P + P] = mx_ref.matmul(mx_ref.quantize(np.ascontiguousarray(cut(w[r], o))), cs[r])
    return {"oc": oc, "osc": osc, "tg": tg, "y": y}

@@ -1,0 +1,450 @@
+from concourse.mybir import dt, AluOpType as Op, AxisListType, ActivationFunctionType as Act
+
+N, P, K, R = 8, 192, 32, 3
+TINY = 1e-30
+BIG = 2.0 ** 30
+LOW = -1e29
+
+MXC, U8, F32, BF, I32, U16 = "float8_e4m3fn_x4", "uint8", "float32", "bfloat16", "int32", "uint16"
+SCRATCH = {}
+
+
+def _buf(name, cols, dtype, where="sbuf"):
+    SCRATCH[name] = (where, [128, cols], dtype)
+
+
+def _pair(name, cols):
+    _buf(name + "q", cols, MXC)
+    _buf(name + "s", cols, U8)
+
+
+for _t in range(R):
+    _pair("x%d" % _t, P)
+    _pair("v%d" % _t, P + 160)
+    _pair("n%d" % _t, K)
+    _pair("u%d" % _t, 320)
+    _buf("sc%d" % _t, 32, F32)
+    _buf("cr%d" % _t, 32, F32)
+    _buf("gi%d" % _t, P, F32)
+_pair("x3", P)
+for _n, _c in (("w", 128), ("eb", 512), ("kc", 512), ("e", 128), ("cm", P), ("mk", P), ("xo", 128), ("wf", 128), ("xf", 128)):
+    _pair(_n, _c)
+for _n, _c in (("ct", 4 * P), ("ut", 16), ("wt", 512), ("ub", 1280), ("st", 2048), ("kst", 2048), ("et", 512), ("cmt", 4 * P),
+               ("mkt", 4 * P), ("zz", 544), ("wft", 512), ("mt", 512), ("oneb", P), ("er", 256), ("cw", 256), ("rb", 128), ("jb", P)):
+    _buf(_n, _c, BF)
+for _n, _c in (("th0", P), ("th1", P), ("thn", P), ("zf", P), ("one32", 32), ("up32", 32), ("eye32", 32), ("mw", 16), ("mwb", 16), ("m8", 8),
+               ("d16", 8), ("dm", 8), ("cf", 16), ("rk", 8), ("ohb", 16), ("oha", 16), ("ohv", 16), ("pm", 200), ("inp", 8), ("tb", 32),
+               ("tt", 32), ("ne", 32), ("mb", 32), ("mr", 32), ("le", 40), ("dg", 32), ("xa", 24), ("hd", 4 * P), ("ha", 128),
+               ("yw", 256), ("yo", P), ("tgb", 16), ("js", 200)):
+    _buf(_n, _c, F32)
+_buf("ic", 16, I32)
+_buf("ol", 2, U16)
+_buf("om", 8, U16)
+_buf("of", 12, U16)
+for _n in range(8):
+    _buf("b%d" % _n, 512, F32, "psum")
+
+SEMAPHORES = ["sv", "ss", "stn", "sg", "lc", "lu", "lw", "oc_", "oy_"] + ["os%d" % k for k in range(4)] + ["tg_%d" % k for k in range(R)] \
+    + ["arr%d" % k for k in range(R)] + ["sent%d" % k for k in range(R)] + ["cq%d" % k for k in range(R)] + ["cs%d" % k for k in range(R)]
+
+
+def _cross(a, b):
+    if a[1] >= b[2] or b[1] >= a[2] or a[3] >= b[4] or b[3] >= a[4]:
+        return False
+    m = min(a[5], b[5])
+    if m > 1 and a[5] % m == 0 and b[5] % m == 0:
+        return (a[3] - b[3]) % m == 0
+    return True
+
+
+def _within(a, b):
+    if not (a[1] <= b[1] and b[2] <= a[2] and a[3] <= b[3] and b[4] <= a[4]):
+        return False
+    return a[5] == 1 or (a[5] == b[5] and (a[3] - b[3]) % a[5] == 0)
+
+
+def rank_program(g, core, T, topo):
+    rank = T.rank_of(core)
+    if rank is None:
+        return
+    queue = {"V": g.vector, "S": g.scalar, "T": g.tensor, "G": g, "Y": g.sync}
+    own = {"V": "sv", "S": "ss", "T": "stn", "G": "sg"}
+    count = {"V": 0, "S": 0, "T": 0, "G": 0}
+    known = {q: {} for q in queue}
+    log = {}
+    every = {}
+    serial = [0]
+
+    def A(name, c0, c1, step=1, p0=0, p1=128):
+        return (name, p0, p1, c0, c1, step)
+
+    def ap(x):
+        return T[x[0]][x[1]:x[2], x[3]:x[4]:x[5]] if x[5] > 1 else T[x[0]][x[1]:x[2], x[3]:x[4]]
+
+    def psum(x):
+        return SCRATCH[x[0]][0] == "psum"
+
+    def need(q, reads, writes):
+        want = []
+        for views, w in ((reads, False), (writes, True)):
+            for x in views:
+                for y, ins, yw in log.get(x[0], []):
+                    if psum(x):
+                        hit = (q != ins["q"]) or (q != "T" and (w or yw))
+                    else:
+                        hit = (w or yw) and _cross(x, y)
+                    if hit:
+                        want.append(ins)
+        for ins in sorted(want, key=lambda i: -i["n"]):
+            if known[q].get(ins["sem"], 0) >= ins["val"]:
+                continue
+            queue[q].wait_ge(T.sem[ins["sem"]], ins["val"])
+            for s, v in list(ins["clock"].items()) + [(ins["sem"], ins["val"])]:
+                known[q][s] = max(known[q].get(s, 0), v)
+
+    def note(q, reads, writes, sem, val):
+        serial[0] += 1
+        ins = {"q": q, "sem": sem, "val": val, "clock": dict(known.get(q, {})), "n": serial[0]}
+        every[sem] = val
+        for x in writes:
+            log[x[0]] = [e for e in log.get(x[0], []) if not _within(x, e[0]) or (psum(x) and q == "T" and e[1]["q"] == "T")]
+        for views, w in ((reads, False), (writes, True)):
+            for x in views:
+                log.setdefault(x[0], []).append((x, ins, w))
+
+    def do(q, reads, writes, call):
+        need(q, reads, writes)
+        count[q] += 1
+        note(q, reads, writes, own[q], count[q])
+        call().then_inc(T.sem[own[q]], 1)
+
+    def dma(q, out, in_, sem, reads, writes):
+        need(q, reads, writes)
+        note(q, reads, writes, sem, 16)
+        queue[q].dma_start(out, in_).then_inc(T.sem[sem], 16)
+
+    V, S = g.vector, g.scalar
+
+    def fill(x, v):
+        do("V", [], [x], lambda: V.memset(ap(x), v))
+
+    def copy(o, i):
+        do("V", [i], [o], lambda: V.tensor_copy(ap(o), ap(i)))
+
+    def ts(o, i, s1, s2, op0, op1=None):
+        rd = [i] + [s for s in (s1, s2) if isinstance(s, tuple)]
+        a, b = (ap(s) if isinstance(s, tuple) else s for s in (s1, s2))
+        if op1 is None:
+            do("V", rd, [o], lambda: V.tensor_scalar(ap(o), ap(i), a, None, op0))
+        else:
+            do("V", rd, [o], lambda: V.tensor_scalar(ap(o), ap(i), a, b, op0, op1))
+
+    def tt(o, i0, i1, op):
+        do("V", [i0, i1], [o], lambda: V.tensor_tensor(ap(o), ap(i0), ap(i1), op))
+
+    def red(o, i, op):
+        do("V", [i], [o], lambda: V.tensor_reduce(ap(o), ap(i), AxisListType.X, op))
+
+    def scan(o, d0, d1, init, op0, op1):
+        do("V", [d0, d1], [o], lambda: V.tensor_tensor_scan(ap(o), ap(d0), ap(d1), init, op0, op1))
+
+    def turn(o, i):
+        do("V", [i], [o], lambda: V.transpose(ap(o), ap(i)))
+
+    def act(o, i, f=Act.Identity, bias=0.0, scale=1.0, acc=None):
+        rd = [i] + [s for s in (bias, scale) if isinstance(s, tuple)]
+        b, c = (ap(s) if isinstance(s, tuple) else s for s in (bias, scale))
+        if acc is None:
+            do("S", rd, [o], lambda: S.activation(ap(o), ap(i), f, bias=b, scale=c))
+        else:
+            do("S", rd, [o, acc], lambda: S.activation(ap(o), ap(i), f, bias=b, scale=c, accum_out=ap(acc)))
+
+    def quant(n, c0, c1, i):
+        q, s = A(n + "q", c0, c1), A(n + "s", c0, c1)
+        do("V", [i], [q, s], lambda: V.quantize_mx(ap(q), ap(s), ap(i)))
+
+    def mm(o, l, r, start=True, stop=True):
+        lq, ls, rq, rs = A(l[0] + "q", l[1], l[2]), A(l[0] + "s", l[1], l[2]), A(r[0] + "q", r[1], r[2]), A(r[0] + "s", r[1], r[2])
+        x = A(o, 0, r[2] - r[1])
+        do("T", [lq, ls, rq, rs], [x], lambda: g.tensor.matmul_mx(ap(x), ap(lq), ap(ls), ap(rq), ap(rs), start, stop))
+
+    def pick_codes(o, i, off):
+        do("V", [i, off], [o], lambda: V.tensor_copy(ap(o).bitcast(dt.uint32), ap(i).bitcast(dt.uint32).indirect(ap(off))))
+
+    def pick_s(o, i, off):
+        do("S", [i, off], [o], lambda: S.activation(ap(o), ap(i).indirect(ap(off)), Act.Copy))
+
+    def pick_v(o, i, off):
+        do("V", [i, off], [o], lambda: V.tensor_copy(ap(o), ap(i).indirect(ap(off))))
+
+    def iota(o, pattern, base, cm):
+        if SCRATCH[o[0]][2] != I32:
+            do("G", [], [o], lambda: g.iota(ap(o), pattern, base, cm, allow_small_or_imprecise_dtypes=True))
+        else:
+            do("G", [], [o], lambda: g.iota(ap(o), pattern, base, cm))
+
+    def sel(o, i, pattern, op, base, cm):
+        do("G", [i], [o], lambda: g.affine_select(ap(o), ap(i), pattern, op, 0.0, base, cm))
+
+    L = 32
+
+    def whole(n, c):
+        return A(n, 0, c)
+
+    def Z(n, c0, c1, step=1):
+        return A(n, c0, c1, step, 0, L)
+
+    def cf(k, p1=128):
+        return A("cf", k, k + 1, 1, 0, p1)
+
+    dma("Y", T.ct[:, :], T.c[:, :], "lc", [], [whole("ct", 4 * P)])
+    dma("S", T.ut[:, 0:16], T.u[:, 0:16], "lu", [], [whole("ut", 16)])
+    dma("Y", T.wt[:, :], T.w[:, :], "lw", [], [whole("wt", 512)])
+
+    fill(whole("zz", 544), 0.0)
+    fill(whole("thn", P), -TINY)
+    fill(whole("oneb", P), 1.0)
+    iota(A("ic", 0, 1), [[0, 1]], 0, 1)
+    iota(whole("er", 256), [[0, 8], [1, 16], [16, 2]], 0, 0)
+    for h in range(2):
+        sel(whole("th%d" % h, P), whole("thn", P), [[-1, P]], Op.is_gt, 64 * h, 1)
+    zero = whole("zz", 512)
+    for x in (A("kst", 0, 512), A("st", 0, 512), A("kst", 512, 1024), A("kst", 1536, 2048)):
+        act(x, zero, Act.Copy)
+    act(A("kst", 1024, 1536), zero, bias=-BIG)
+    for x in (whole("wft", 512), whole("mt", 512)):
+        act(x, zero, Act.Copy)
+    ts(A("ic", 1, 2), A("ic", 0, 1), 112, None, Op.bitwise_and)
+    ts(A("ic", 2, 3), A("ic", 0, 1), 15, None, Op.bitwise_and)
+    copy(A("cf", 0, 2), A("ic", 1, 3))
+    fill(whole("zf", P), 0.0)
+    ts(cf(2), cf(0), 64.0, None, Op.add)
+    copy(cf(3), cf(1))
+    fill(A("cf", 2, 4, 1, 0, 64), 0.0)
+    for e, k in ((0, 0), (6, 0), (8, 1), (14, 1)):
+        copy(A("kst", e, e + 2), A("cf", k, 4, 2))
+    quant("kc", 0, 128, A("kst", 0, 512))
+
+    def query(t):
+        for b in range(4):
+            one = A("ut", 4 * t + b, 4 * t + b + 1)
+            if t == 0:
+                ts(A("ub", 512 + b, 1280, 4), A("oneb", 0, P), one, None, Op.mult)
+            else:
+                act(A("ub", 512 + b, 1280, 4), whole("zf", P), bias=one)
+        if t == 0:
+            quant("u0", 128, 320, A("ub", 512, 1280))
+        for b in range(4):
+            one = A("ut", 4 * t + b, 4 * t + b + 1)
+            ts(A("ub", b, 512, 4), A("oneb", 0, 128), one, -1.0, Op.mult, Op.mult)
+        if t == 0:
+            quant("x0", 0, P, whole("ct", 4 * P))
+            quant("u0", 0, 128, A("ub", 0, 512))
+        else:
+            quant("u%d" % t, 0, 320, whole("ub", 1280))
+
+    query(0)
+    fill(A("cmt", 2, 4 * P, 4), 0.0)
+    fill(A("cmt", 3, 4 * P, 4), 0.0)
+    for t in range(R):
+        quant("v%d" % t, P + K, P + 160, zero)
+    fill(Z("one32", 0, 32), 1.0)
+    fill(Z("pm", 0, 1), LOW)
+    iota(whole("cw", 256), [[0, 8], [1, 16], [0, 2]], 1, 0)
+    iota(whole("mw", 12), [[1, 12]], 0, 0)
+    iota(Z("mwb", 0, 12), [[2, 12]], -12, 0)
+    sel(A("st", 0, 512, 4), A("oneb", 0, 128), [[-1, 128]], Op.is_equal, 0, 1)
+    iota(whole("rb", 128), [[0, 8], [1, 4], [0, 4]], 0, 0)
+    iota(Z("m8", 0, 8), [[1, 8]], 0, 0)
+    sel(Z("up32", 0, 32), Z("one32", 0, 32), [[1, 32]], Op.is_gt, 0, -1)
+    sel(Z("eye32", 0, 32), Z("one32", 0, 32), [[1, 32]], Op.is_equal, 0, -1)
+    JT, ONES, NEG, W1 = ("kc", 0, 128), ("kc", 128, 256), ("kc", 256, 384), ("kc", 384, 512)
+
+    def columns():
+        for k, m in ((3, 3), (4, 31), (6, 16)):
+            ts(A("ic", k, k + 1), A("ic", 0, 1), m, None, Op.bitwise_and)
+        ts(A("ic", 5, 6), A("ic", 4, 5), 2, None, Op.arith_shift_right)
+        fill(A("kst", 512, 1024, 4), 1.0)
+        fill(A("kst", 513, 1024, 4, 64, 128), 1.0)
+        copy(A("cf", 4, 8), A("ic", 3, 7))
+        ts(cf(10), cf(1), 1.0, None, Op.add)
+        ts(cf(8), cf(5), 0.5, None, Op.add)
+        ts(cf(9), cf(7), 224.0, None, Op.add)
+        for b in range(2):
+            ts(Z("kst", 1536 + b, 2048, 4), Z("rb", 0, 128), cf(4, L), None, Op.is_equal)
+        quant("kc", 128, 512, A("kst", 512, 2048))
+
+    def decoders():
+        for b in range(1, 4):
+            act(A("st", 512 * b + b, 512 * b + 512, 4), A("st", 0, 512, 4), Act.Copy)
+        quant("eb", 0, 512, whole("st", 2048))
+
+    def later():
+        ts(Z("d16", 0, 8), Z("m8", 0, 8), cf(6, L), 16.0, Op.is_equal, Op.mult)
+        ts(Z("dm", 0, 8), Z("m8", 0, 8), cf(6, L), -1000.0, Op.not_equal, Op.mult)
+        ts(Z("dm", 0, 8), Z("dm", 0, 8), -0.0625, None, Op.add)
+        fill(A("wft", 0, 512, 4, 32, 33), 1.0)
+        ts(A("wft", 2, 512, 4, 32, 33), A("cw", 0, 256, 2, 32, 33), -1.0, None, Op.add)
+        ts(A("zz", 32, 80, 4, 32, 33), A("mw", 0, 12, 1, 32, 33), 16.0, None, Op.mult)
+        fill(A("zz", 34, 80, 4, 32, 33), 1.0)
+
+    def place(t, part):
+        c = "sc%d" % t
+
+        def sc(k):
+            return Z(c, k, k + 1)
+        if part == 1:
+            tt(Z("dg", 0, 32), Z("cr%d" % t, 0, 32), Z("eye32", 0, 32), Op.mult)
+            red(sc(20), Z("dg", 0, 32), Op.add)
+            ts(sc(21), sc(20), -0.5, None, Op.add)
+            act(Z("js", 0, P), Z("gi%d" % t, 0, P), Act.Sign, bias=sc(21), scale=-1.0 / BIG, acc=sc(22))
+        else:
+            ts(sc(23), sc(22), -0.5, -97.0, Op.mult, Op.add)
+            ts(sc(24), sc(1), sc(23), 1.0, Op.subtract, Op.subtract)
+            ts(Z("tgb", t, t + 1), sc(24), sc(5), sc(23), Op.mult, Op.add)
+            dma("Y", T.tg[t:t + 1, :], T.tgb[0:L, t:t + 1], "tg_%d" % t, [Z("tgb", t, t + 1)], [])
+
+    for t in range(R):
+        x, v, n, u, nx, c, cr, gi = "x%d" % t, "v%d" % t, "n%d" % t, "u%d" % t, "x%d" % (t + 1), "sc%d" % t, "cr%d" % t, "gi%d" % t
+        last = t == R - 1
+
+        def sc(k):
+            return Z(c, k, k + 1)
+        for h in range(2):
+            mm("b%d" % h, (x, 64 * h, 64 * h + 128), (u, 128, 320), True, False)
+            mm("b%d" % h, (u, 0, 128), (x, 0, P), False, True)
+        if t > 0:
+            place(t - 1, 1)
+        tt(A("cmt", 0, 4 * P, 4), A("b0", 0, P), whole("th0", P), Op.is_gt)
+        if t == 0:
+            act(A("st", 512, 1024), A("kst", 0, 512), Act.Copy, scale=0.0)
+        act(whole("jb", P), A("cmt", 0, 4 * P, 4), Act.Copy, acc=A("rk", 0, 1))
+        if t == 0:
+            for b in (2, 3):
+                act(A("st", 512 * b, 512 * b + 512), A("kst", 0, 512), Act.Copy, scale=0.0)
+        tt(A("cmt", 1, 4 * P, 4), A("b1", 0, P), whole("th1", P), Op.is_gt)
+        red(A("rk", 1, 2), A("cmt", 1, 4 * P, 4), Op.add)
+        for h in range(2):
+            ts(A("et", h, 512, 2), whole("er", 256), A("rk", h, h + 1), None, Op.is_equal)
+        quant("e", 0, 128, whole("et", 512))
+        mm("b2", ("e", 0, 128), JT)
+        quant("cm", 0, P, whole("cmt", 4 * P))
+        for m in range(2):
+            ts(A("ol", m, m + 1), A("b2", m, m + 1), A("b2", m + 2, m + 3), None, Op.add)
+        pick_codes(A(n + "q", 0, K), A(x + "q", 0, P), A("ol", 0, 2))
+        pick_s(A(n + "s", 0, K), A(x + "s", 0, P), A("ol", 0, 2))
+        dst = T.cores[rank ^ (1 << t)]
+        rid, pid = topo.addr(dst, core)
+        mask, en = topo.mask(core, dst), len(topo.engines(core, dst))
+        need("G", [A(n + "q", 0, K)], [])
+        g.remote_dma(T[v + "q"][:, P:P + K].bitcast(dt.uint8), T[n + "q"][:, 0:K].bitcast(dt.uint8), T.sem["arr%d" % t], T.sem["sent%d" % t], pid, rid, mask)
+        need("G", [A(n + "s", 0, K)], [])
+        g.remote_dma(T[v + "s"][:, P:P + K], T[n + "s"][:, 0:K], T.sem["arr%d" % t], T.sem["sent%d" % t], pid, rid, mask)
+        note("arrive", [], [A(v + "q", P, P + K), A(v + "s", P, P + K)], "arr%d" % t, 2 * en)
+        every["sent%d" % t] = 2 * en
+        dma("Y", T[v + "q"][:, 0:P].bitcast(dt.uint8), T[x + "q"][:, 0:P].bitcast(dt.uint8), "cq%d" % t, [A(x + "q", 0, P)], [A(v + "q", 0, P)])
+        dma("Y", T[v + "s"][:, 0:P], T[x + "s"][:, 0:P], "cs%d" % t, [A(x + "s", 0, P)], [A(v + "s", 0, P)])
+        if t == 0:
+            columns()
+            decoders()
+        mm("b4", ONES, ("cm", 0, P))
+        ts(A("mkt", 0, 4 * P, 4), A("b4", 0, P), 159.5, BIG, Op.is_gt, Op.mult)
+        copy(A("mkt", 1, 4 * P, 4), A("mkt", 0, 4 * P, 4))
+        act(A("mkt", 2, 4 * P, 4), A("mkt", 0, 4 * P, 4), Act.Copy)
+        copy(A("mkt", 3, 4 * P, 4), A("mkt", 0, 4 * P, 4))
+        scan(Z(gi, 0, P), Z("mkt", 0, 4 * P, 4), Z("zf", 0, P), 0.0, Op.add, Op.add)
+        quant("mk", 0, P, whole("mkt", 4 * P))
+        act(Z("js", 0, 12), Z(gi, 15, P, 16), Act.Sign, bias=cf(8, L), scale=-1.0 / BIG, acc=sc(10))
+        act(Z("js", 0, P), Z(gi, 0, P), Act.Sign, bias=cf(8, L), scale=-1.0 / BIG, acc=sc(11))
+        if t == 0:
+            later()
+        for b in range(4):
+            bank = ("b6", "b7", "b0", "b1")[b]
+            mm(bank, ("eb", 128 * b, 128 * b + 128), (x, 0, P))
+            act(A("hd", b, 4 * P, 4), A(bank, 0, P), Act.Copy, scale=0.5)
+        for k in range(4):
+            mm("b5", NEG, ("mk", 0, P), k == 0, False)
+        ts(Z("ohb", 0, 12), Z("mwb", 0, 12), sc(10), None, Op.is_equal)
+        ts(sc(12), sc(10), -8.0, 96.0, Op.mult, Op.add)
+        ts(sc(13), sc(10), -16.0, sc(11), Op.mult, Op.add)
+        ts(sc(14), sc(13), 0.5, 1.0, Op.mult, Op.add)
+        ts(Z("le", 32, 33), sc(13), -0.5, None, Op.mult)
+        ts(Z("wft", 1, 512, 2), Z("cw", 0, 256), sc(14), None, Op.is_equal)
+        if t == 0:
+            quant("w", 0, 128, whole("wt", 512))
+        if not last:
+            query(t + 1)
+        else:
+            mm("b2", ("w", 0, 128), (x, 0, P))
+            act(A("yw", 0, P), A("b2", 0, P), Act.Copy)
+        if t > 0:
+            place(t - 1, 2)
+
+        mm("b5", (v, P, P + 128), (x, 0, P), False, True)
+        for b in range(4):
+            mm(("b6", "b7", "b4", "b1")[b], ("eb", 128 * b, 128 * b + 128), (v, P, P + 128))
+
+        def half(b):
+            act(A("ha", b, 128, 4), A(("b6", "b7", "b4", "b1")[b], 0, K), Act.Copy, scale=0.5)
+        scan(Z("pm", 1, 1 + P), A("b5", 0, P, 1, 0, L), Z("zf", 0, P), LOW, Op.max, Op.add)
+        top = Z("pm", P, P + 1)
+        half(0)
+        act(Z("js", 0, 12), Z("pm", 16, 1 + P, 16), Act.Sign, bias=top, scale=-1.0, acc=sc(0))
+        act(Z("js", 0, 1 + P), Z("pm", 0, 1 + P), Act.Sign, bias=top, scale=-1.0, acc=sc(1))
+        ts(Z("inp", 0, 8), Z("dm", 0, 8), sc(0), 16.0, Op.subtract, Op.mult)
+        ts(Z("zz", 0, 32, 4), Z("d16", 0, 8), sc(0), None, Op.mult)
+        ts(Z("oha", 0, 12), Z("mw", 0, 12), sc(0), None, Op.is_equal)
+        ts(sc(2), sc(0), -16.0, cf(9, L), Op.mult, Op.add)
+        act(Z("tb", 0, 32), Z("up32", 0, 32), scale=sc(1))
+        act(sc(3), sc(0), scale=-16.0, bias=sc(1))
+        act(Z("xa", 0, 24, 2), Z("oha", 0, 12), scale=sc(2))
+        act(sc(4), sc(3), scale=-1.0, bias=cf(10, L))
+        half(1)
+        act(Z("xa", 1, 24, 2), Z("oha", 0, 12), scale=sc(4))
+        half(2)
+        half(3)
+        ts(Z("zz", 1, 32, 4), Z("inp", 0, 8), sc(1), 0.0, Op.add, Op.max)
+        turn(Z("tt", 0, 32), Z("tb", 0, 32))
+        quant("xo", 0, 128, A("zz", 0, 512))
+        mm("b3", W1, ("xo", 0, 128))
+        ts(Z("ne", 0, 32), Z("tt", 0, 32), sc(1), None, Op.not_equal)
+        ts(Z("wft", 0, 512, 2), Z("cw", 0, 256), sc(3), None, Op.is_equal)
+        red(sc(5), Z("ne", 0, 32), Op.min)
+        act(Z("mb", 0, 32), Z("one32", 0, 32), scale=sc(5))
+        act(Z("zz", 32, 80, 2), Z("xa", 0, 24), scale=sc(5))
+        quant("wf", 0, 128, whole("wft", 512))
+        ts(A("om", 0, 8), A("b3", 0, 8), 4.0, cf(4), Op.mult, Op.add)
+        turn(Z("mr", 0, 32), Z("mb", 0, 32))
+        scan(Z(cr, 0, 32), Z("one32", 0, 32), Z("mr", 0, 32), 0.0, Op.add, Op.subtract)
+        ts(Z("le", 0, 32), Z(cr, 0, 32), cf(5, L), None, Op.is_le)
+        ts(Z("le", 33, 34), Z(cr, 15, 16), cf(5, L), -16.0, Op.is_le, Op.mult)
+        ts(sc(6), Z(cr, 31, 32), cf(5, L), None, Op.is_gt)
+        red(sc(7), Z("le", 0, 34), Op.add)
+        ts(Z("ohv", 0, 12), Z("ohb", 0, 12), sc(6), None, Op.mult)
+        act(sc(8), Z("le", 33, 34), scale=-1.0, bias=sc(12))
+        act(Z("zz", 33, 80, 4), Z("ohv", 0, 12), scale=sc(8))
+        ts(Z("zz", 35, 80, 4), Z("ohb", 0, 12), sc(7), sc(6), Op.mult, Op.mult)
+        quant("xf", 0, 128, A("zz", 32, 544))
+        mm("b2", ("wf", 0, 128), ("xf", 0, 128))
+        ho, hi_, of, ha = A("mt", 0, 128), A("hd", 0, 4 * P), A("om", 0, 8), A("ha", 0, 128)
+        do("V", [hi_, of, ha], [ho], lambda: V.tensor_tensor(ap(ho), ap(hi_).indirect(ap(of)), ap(ha), Op.add))
+        quant(v, P + K, P + 160, whole("mt", 512))
+        copy(A("of", 0, 12), A("b2", 0, 12))
+        if not last:
+            for a, b in ((0, 8), (8, 12)):
+                pick_codes(A(nx + "q", 16 * a, 16 * b), A(v + "q", 0, 256), A("of", a, b))
+                pick_s(A(nx + "s", 16 * a, 16 * b), A(v + "s", 0, 256), A("of", a, b))
+        else:
+            mm("b3", ("w", 0, 128), (v, P, P + 128))
+            act(A("yw", P, P + 64), A("b3", 0, 64), Act.Copy)
+            pick_codes(A(nx + "q", 0, P), A(v + "q", 0, 256), A("of", 0, 12))
+            pick_s(A("yo", 0, P), A("yw", 0, 256), A("of", 0, 12))
+            dma("Y", T.oc[:, :], T.x3q[:, 0:P].bitcast(dt.uint8), "oc_", [A("x3q", 0, P)], [])
+            dma("S", T.y[:, :], T.yo[:, 0:P], "oy_", [A("yo", 0, P)], [])
+            place(t, 1)
+            pick_v(A(nx + "s", 0, P), A(v + "s", 0, 256), A("of", 0, 12))
+            for k in range(4):
+                dma("Y", T.osc[4 * k:4 * k + 4, :], T.x3s[32 * k:32 * k + 4, 0:P], "os%d" % k, [A("x3s", 0, P)], [])
+            place(t, 2)
+    for s in every:
+        g.wait_ge(T.sem[s], every[s])

@@ -4,6 +4,7 @@ N, P, K, R = 8, 192, 32, 3
 TINY = 1e-30
 BIG = 2.0 ** 30
 LOW = -1e29
+WAKE, SLACK = 0.1, 0.3
 
 MXC, U8, F32, BF, I32, U16 = "float8_e4m3fn_x4", "uint8", "float32", "bfloat16", "int32", "uint16"
 SCRATCH = {}
@@ -30,10 +31,10 @@ _pair("x3", P)
 for _n, _c in (("w", 128), ("eb", 512), ("kc", 512), ("e", 128), ("cm", P), ("mk", P), ("xo", 128), ("wf", 128), ("xf", 128)):
     _pair(_n, _c)
 for _n, _c in (("ct", 4 * P), ("ut", 16), ("wt", 512), ("ub", 1280), ("st", 2048), ("kst", 2048), ("et", 512), ("cmt", 4 * P),
-               ("mkt", 4 * P), ("zz", 544), ("wft", 512), ("mt", 512), ("oneb", P), ("er", 256), ("cw", 256), ("rb", 128), ("jb", P)):
+               ("mkt", 4 * P), ("zz", 544), ("wft", 512), ("mt", 512), ("oneb", P), ("er", 256), ("cw", 256), ("rb", 128), ("rk0", P), ("rk1", P)):
     _buf(_n, _c, BF)
 for _n, _c in (("th0", P), ("th1", P), ("thn", P), ("zf", P), ("one32", 32), ("up32", 32), ("eye32", 32), ("mw", 16), ("mwb", 16), ("m8", 8),
-               ("d16", 8), ("dm", 8), ("cf", 16), ("rk", 8), ("ohb", 16), ("oha", 16), ("ohv", 16), ("pm", 200), ("inp", 8), ("tb", 32),
+               ("d16", 8), ("dm", 8), ("cf", 16), ("ohb", 16), ("oha", 16), ("ohv", 16), ("pm", 200), ("inp", 8), ("tb", 32), ("hp", 16),
                ("tt", 32), ("ne", 32), ("mb", 32), ("mr", 32), ("le", 40), ("dg", 32), ("xa", 24), ("hd", 4 * P), ("ha", 128),
                ("yw", 256), ("yo", P), ("tgb", 16), ("js", 200)):
     _buf(_n, _c, F32)
@@ -63,17 +64,56 @@ def _within(a, b):
     return a[5] == 1 or (a[5] == b[5] and (a[3] - b[3]) % a[5] == 0)
 
 
+def _size(x):
+    return (x[4] - x[3] + x[5] - 1) // x[5]
+
+
+def _order(nodes):
+    users = [[] for m in nodes]
+    for m in nodes:
+        for d in m["after"]:
+            users[d].append(m["n"])
+    way = [0.0] * len(nodes)
+    for m in reversed(nodes):
+        way[m["n"]] = max([m["late"]] + [m["late"] + WAKE * nodes[k]["after"][m["n"]] + way[k] for k in users[m["n"]]])
+    left = [len(m["after"]) for m in nodes]
+    ready = [0.0] * len(nodes)
+    free = {}
+    able = [m["n"] for m in nodes if not m["after"]]
+    done = []
+    while able:
+        best = None
+        for q in set(nodes[k]["q"] for k in able):
+            ks = [k for k in able if nodes[k]["q"] == q]
+            t0 = max(free.get(q, 0.0), min(ready[k] for k in ks))
+            ks = [k for k in ks if ready[k] <= t0 + SLACK]
+            k = max(ks, key=lambda i: (way[i], -i))
+            now = [i for i in ks if ready[i] <= t0 and t0 + 1.8 * nodes[i]["busy"] <= ready[k] + 0.02]
+            if ready[k] > t0 and now:
+                k = max(now, key=lambda i: (way[i], -i))
+            t = max(t0, ready[k])
+            if best is None or (t, q) < best[:2]:
+                best = (t, q, k)
+        t, q, k = best
+        able.remove(k)
+        free[q] = t + nodes[k]["busy"]
+        done.append(k)
+        for i in users[k]:
+            ready[i] = max(ready[i], t + nodes[k]["late"] + (WAKE if nodes[i]["after"][k] else 0.0))
+            left[i] -= 1
+            if not left[i]:
+                able.append(i)
+    return done
+
+
 def rank_program(g, core, T, topo):
     rank = T.rank_of(core)
     if rank is None:
         return
     queue = {"V": g.vector, "S": g.scalar, "T": g.tensor, "G": g, "Y": g.sync}
     own = {"V": "sv", "S": "ss", "T": "stn", "G": "sg"}
-    count = {"V": 0, "S": 0, "T": 0, "G": 0}
-    known = {q: {} for q in queue}
     log = {}
-    every = {}
-    serial = [0]
+    nodes = []
 
     def A(name, c0, c1, step=1, p0=0, p1=128):
         return (name, p0, p1, c0, c1, step)
@@ -84,44 +124,75 @@ def rank_program(g, core, T, topo):
     def psum(x):
         return SCRATCH[x[0]][0] == "psum"
 
-    def need(q, reads, writes):
-        want = []
+    def add(q, reads, writes, busy, late, issue, sem=None, val=0):
+        after = {}
+        node = {"q": q, "n": len(nodes), "after": after, "busy": busy, "late": late, "issue": issue, "sem": sem, "val": val}
         for views, w in ((reads, False), (writes, True)):
             for x in views:
-                for y, ins, yw in log.get(x[0], []):
+                for y, m, yw in log.get(x[0], []):
                     if psum(x):
-                        hit = (q != ins["q"]) or (q != "T" and (w or yw))
-                    else:
-                        hit = (w or yw) and _cross(x, y)
-                    if hit:
-                        want.append(ins)
-        for ins in sorted(want, key=lambda i: -i["n"]):
-            if known[q].get(ins["sem"], 0) >= ins["val"]:
-                continue
-            queue[q].wait_ge(T.sem[ins["sem"]], ins["val"])
-            for s, v in list(ins["clock"].items()) + [(ins["sem"], ins["val"])]:
-                known[q][s] = max(known[q].get(s, 0), v)
-
-    def note(q, reads, writes, sem, val):
-        serial[0] += 1
-        ins = {"q": q, "sem": sem, "val": val, "clock": dict(known.get(q, {})), "n": serial[0]}
-        every[sem] = val
+                        if q == "T" and m["q"] == "T":
+                            after.setdefault(m["n"], False)
+                        elif q != m["q"] or w or yw:
+                            after[m["n"]] = True
+                    elif (w or yw) and _cross(x, y):
+                        after[m["n"]] = True
         for x in writes:
             log[x[0]] = [e for e in log.get(x[0], []) if not _within(x, e[0]) or (psum(x) and q == "T" and e[1]["q"] == "T")]
         for views, w in ((reads, False), (writes, True)):
             for x in views:
-                log.setdefault(x[0], []).append((x, ins, w))
+                log.setdefault(x[0], []).append((x, node, w))
+        nodes.append(node)
+        return node
 
-    def do(q, reads, writes, call):
-        need(q, reads, writes)
-        count[q] += 1
-        note(q, reads, writes, own[q], count[q])
-        call().then_inc(T.sem[own[q]], 1)
+    def do(q, reads, writes, call, kind=""):
+        n = max(_size(x) for x in reads[:1] + writes[:1])
+        if kind == "quant":
+            cost = 0.015 + 0.000275 * _size(reads[0])
+        elif kind == "pick":
+            cost = 0.07 + 0.0016 * _size(writes[0])
+        elif q == "T":
+            cost = 0.0015 * (_size(writes[0]) + 16)
+        elif q == "G":
+            cost = 0.2 + 0.002 * n
+        else:
+            two = q == "V" and all(SCRATCH[x[0]][2] in (BF, U16) for x in reads[:1] + writes[:1])
+            cost = max(64, n * (0.5 if two else 1)) * 0.00104
+        return add(q, reads, writes, cost, cost, call)
 
     def dma(q, out, in_, sem, reads, writes):
-        need(q, reads, writes)
-        note(q, reads, writes, sem, 16)
-        queue[q].dma_start(out, in_).then_inc(T.sem[sem], 16)
+        add(q, reads, writes, 0.1, 2.2, lambda: queue[q].dma_start(out, in_), sem, 16)
+
+    def emit():
+        count = {"V": 0, "S": 0, "T": 0, "G": 0}
+        known = {q: {} for q in queue}
+        every = {}
+        done = _order(nodes)
+        at = {k: i for i, k in enumerate(done)}
+        for k in done:
+            m = nodes[k]
+            q = m["q"]
+            if q in queue:
+                for d in sorted(m["after"], reverse=True, key=lambda i: at[i]):
+                    o = nodes[d]
+                    if not m["after"][d] or known[q].get(o["sem"], 0) >= o["val"]:
+                        continue
+                    queue[q].wait_ge(T.sem[o["sem"]], o["val"])
+                    for s, v in list(o["clock"].items()) + [(o["sem"], o["val"])]:
+                        known[q][s] = max(known[q].get(s, 0), v)
+            if m["sem"] is None:
+                count[q] += 1
+                m["sem"], m["val"] = own[q], count[q]
+                m["issue"]().then_inc(T.sem[own[q]], 1)
+            elif m["issue"] is not None:
+                ins = m["issue"]()
+                if m["sem"][0:4] != "sent":
+                    ins.then_inc(T.sem[m["sem"]], 16)
+            m["clock"] = dict(known.get(q, {}))
+            every[m["sem"]] = max(m["val"], every.get(m["sem"], 0))
+        final = ["sg", "stn", "ss", "sv"] + ["os%d" % k for k in range(4)] + ["tg_%d" % (R - 1), "oc_", "oy_"]
+        for s in [e for e in every if e not in final] + final:
+            g.wait_ge(T.sem[s], every[s])
 
     V, S = g.vector, g.scalar
 
@@ -161,21 +232,21 @@ def rank_program(g, core, T, topo):
 
     def quant(n, c0, c1, i):
         q, s = A(n + "q", c0, c1), A(n + "s", c0, c1)
-        do("V", [i], [q, s], lambda: V.quantize_mx(ap(q), ap(s), ap(i)))
+        do("V", [i], [q, s], lambda: V.quantize_mx(ap(q), ap(s), ap(i)), "quant")
 
     def mm(o, l, r, start=True, stop=True):
         lq, ls, rq, rs = A(l[0] + "q", l[1], l[2]), A(l[0] + "s", l[1], l[2]), A(r[0] + "q", r[1], r[2]), A(r[0] + "s", r[1], r[2])
         x = A(o, 0, r[2] - r[1])
-        do("T", [lq, ls, rq, rs], [x], lambda: g.tensor.matmul_mx(ap(x), ap(lq), ap(ls), ap(rq), ap(rs), start, stop))
+        return do("T", [lq, ls, rq, rs], [x], lambda: g.tensor.matmul_mx(ap(x), ap(lq), ap(ls), ap(rq), ap(rs), start, stop))
 
     def pick_codes(o, i, off):
-        do("V", [i, off], [o], lambda: V.tensor_copy(ap(o).bitcast(dt.uint32), ap(i).bitcast(dt.uint32).indirect(ap(off))))
+        do("V", [i, off], [o], lambda: V.tensor_copy(ap(o).bitcast(dt.uint32), ap(i).bitcast(dt.uint32).indirect(ap(off))), "pick")
 
     def pick_s(o, i, off):
-        do("S", [i, off], [o], lambda: S.activation(ap(o), ap(i).indirect(ap(off)), Act.Copy))
+        do("S", [i, off], [o], lambda: S.activation(ap(o), ap(i).indirect(ap(off)), Act.Copy), "pick")
 
     def pick_v(o, i, off):
-        do("V", [i, off], [o], lambda: V.tensor_copy(ap(o), ap(i).indirect(ap(off))))
+        do("V", [i, off], [o], lambda: V.tensor_copy(ap(o), ap(i).indirect(ap(off))), "pick")
 
     def iota(o, pattern, base, cm):
         if SCRATCH[o[0]][2] != I32:
@@ -310,22 +381,22 @@ def rank_program(g, core, T, topo):
 
         def sc(k):
             return Z(c, k, k + 1)
+        pair = []
         for h in range(2):
-            mm("b%d" % h, (x, 64 * h, 64 * h + 128), (u, 128, 320), True, False)
-            mm("b%d" % h, (u, 0, 128), (x, 0, P), False, True)
+            pair.append(mm("b%d" % h, (x, 64 * h, 64 * h + 128), (u, 128, 320), True, False))
+            pair.append(mm("b%d" % h, (u, 0, 128), (x, 0, P), False, True))
+        pair[2]["after"].setdefault(pair[1]["n"], False)
         if t > 0:
             place(t - 1, 1)
         tt(A("cmt", 0, 4 * P, 4), A("b0", 0, P), whole("th0", P), Op.is_gt)
         if t == 0:
-            act(A("st", 512, 1024), A("kst", 0, 512), Act.Copy, scale=0.0)
-        act(whole("jb", P), A("cmt", 0, 4 * P, 4), Act.Copy, acc=A("rk", 0, 1))
-        if t == 0:
-            for b in (2, 3):
+            for b in (1, 2, 3):
                 act(A("st", 512 * b, 512 * b + 512), A("kst", 0, 512), Act.Copy, scale=0.0)
-        tt(A("cmt", 1, 4 * P, 4), A("b1", 0, P), whole("th1", P), Op.is_gt)
-        red(A("rk", 1, 2), A("cmt", 1, 4 * P, 4), Op.add)
         for h in range(2):
-            ts(A("et", h, 512, 2), whole("er", 256), A("rk", h, h + 1), None, Op.is_equal)
+            if h == 1:
+                tt(A("cmt", 1, 4 * P, 4), A("b1", 0, P), whole("th1", P), Op.is_gt)
+            scan(A("rk%d" % h, 0, P), A("cmt", h, 4 * P, 4), A("zz", 80, 80 + P), 0.0, Op.add, Op.add)
+            ts(A("et", h, 512, 2), whole("er", 256), A("rk%d" % h, P - 1, P), None, Op.is_equal)
         quant("e", 0, 128, whole("et", 512))
         mm("b2", ("e", 0, 128), JT)
         quant("cm", 0, P, whole("cmt", 4 * P))
@@ -336,12 +407,13 @@ def rank_program(g, core, T, topo):
         dst = T.cores[rank ^ (1 << t)]
         rid, pid = topo.addr(dst, core)
         mask, en = topo.mask(core, dst), len(topo.engines(core, dst))
-        need("G", [A(n + "q", 0, K)], [])
-        g.remote_dma(T[v + "q"][:, P:P + K].bitcast(dt.uint8), T[n + "q"][:, 0:K].bitcast(dt.uint8), T.sem["arr%d" % t], T.sem["sent%d" % t], pid, rid, mask)
-        need("G", [A(n + "s", 0, K)], [])
-        g.remote_dma(T[v + "s"][:, P:P + K], T[n + "s"][:, 0:K], T.sem["arr%d" % t], T.sem["sent%d" % t], pid, rid, mask)
-        note("arrive", [], [A(v + "q", P, P + K), A(v + "s", P, P + K)], "arr%d" % t, 2 * en)
-        every["sent%d" % t] = 2 * en
+        to = (T.sem["arr%d" % t], T.sem["sent%d" % t], pid, rid, mask)
+        vq, nq, vs, ns = T[v + "q"][:, P:P + K], T[n + "q"][:, 0:K], T[v + "s"][:, P:P + K], T[n + "s"][:, 0:K]
+        m1 = add("G", [A(n + "q", 0, K)], [], 0.9, 0.9, lambda vq=vq, nq=nq, to=to: g.remote_dma(vq.bitcast(dt.uint8), nq.bitcast(dt.uint8), *to), "sent%d" % t, 2 * en)
+        m2 = add("G", [A(n + "s", 0, K)], [], 0.9, 0.9, lambda vs=vs, ns=ns, to=to: g.remote_dma(vs, ns, *to), "sent%d" % t, 2 * en)
+        m2["after"][m1["n"]] = False
+        fly = add("arrive", [], [A(v + "q", P, P + K), A(v + "s", P, P + K)], 1.6, 1.6, None, "arr%d" % t, 2 * en)
+        fly["after"].update({m1["n"]: False, m2["n"]: False})
         dma("Y", T[v + "q"][:, 0:P].bitcast(dt.uint8), T[x + "q"][:, 0:P].bitcast(dt.uint8), "cq%d" % t, [A(x + "q", 0, P)], [A(v + "q", 0, P)])
         dma("Y", T[v + "s"][:, 0:P], T[x + "s"][:, 0:P], "cs%d" % t, [A(x + "s", 0, P)], [A(v + "s", 0, P)])
         if t == 0:
@@ -389,7 +461,8 @@ def rank_program(g, core, T, topo):
         scan(Z("pm", 1, 1 + P), A("b5", 0, P, 1, 0, L), Z("zf", 0, P), LOW, Op.max, Op.add)
         top = Z("pm", P, P + 1)
         half(0)
-        act(Z("js", 0, 12), Z("pm", 16, 1 + P, 16), Act.Sign, bias=top, scale=-1.0, acc=sc(0))
+        ts(Z("hp", 0, 12), Z("pm", 16, 1 + P, 16), top, None, Op.is_lt)
+        red(sc(0), Z("hp", 0, 12), Op.add)
         act(Z("js", 0, 1 + P), Z("pm", 0, 1 + P), Act.Sign, bias=top, scale=-1.0, acc=sc(1))
         ts(Z("inp", 0, 8), Z("dm", 0, 8), sc(0), 16.0, Op.subtract, Op.mult)
         ts(Z("zz", 0, 32, 4), Z("d16", 0, 8), sc(0), None, Op.mult)
@@ -427,7 +500,7 @@ def rank_program(g, core, T, topo):
         quant("xf", 0, 128, A("zz", 32, 544))
         mm("b2", ("wf", 0, 128), ("xf", 0, 128))
         ho, hi_, of, ha = A("mt", 0, 128), A("hd", 0, 4 * P), A("om", 0, 8), A("ha", 0, 128)
-        do("V", [hi_, of, ha], [ho], lambda: V.tensor_tensor(ap(ho), ap(hi_).indirect(ap(of)), ap(ha), Op.add))
+        do("V", [hi_, of, ha], [ho], lambda: V.tensor_tensor(ap(ho), ap(hi_).indirect(ap(of)), ap(ha), Op.add), "pick")
         quant(v, P + K, P + 160, whole("mt", 512))
         copy(A("of", 0, 12), A("b2", 0, 12))
         if not last:
@@ -446,5 +519,4 @@ def rank_program(g, core, T, topo):
             for k in range(4):
                 dma("Y", T.osc[4 * k:4 * k + 4, :], T.x3s[32 * k:32 * k + 4, 0:P], "os%d" % k, [A("x3s", 0, P)], [])
             place(t, 2)
-    for s in every:
-        g.wait_ge(T.sem[s], every[s])
+    emit()

@@ -4,7 +4,9 @@ N, P, K, R = 8, 192, 32, 3
 TINY = 1e-30
 BIG = 2.0 ** 30
 LOW = -1e29
-WAKE, SLACK = 0.1, 0.3
+WAKE, SLACK = 0.18, 0.3
+LOAD, ISSUE, FLIGHT = 1.1, 0.4, 1.0
+MMC = 0.0012
 
 MXC, U8, F32, BF, I32, U16 = "float8_e4m3fn_x4", "uint8", "float32", "bfloat16", "int32", "uint16"
 SCRATCH = {}
@@ -25,8 +27,8 @@ for _t in range(R):
     _pair("n%d" % _t, K)
     _pair("u%d" % _t, 320)
     _buf("sc%d" % _t, 32, F32)
-    _buf("cr%d" % _t, 32, F32)
-    _buf("gi%d" % _t, P, F32)
+    _buf("cr%d" % _t, 64, F32)
+    _buf("gi%d" % _t, P, BF)
 _pair("x3", P)
 for _n, _c in (("w", 128), ("eb", 512), ("kc", 512), ("e", 128), ("cm", P), ("mk", P), ("xo", 128), ("wf", 128), ("xf", 128)):
     _pair(_n, _c)
@@ -34,9 +36,9 @@ for _n, _c in (("ct", 4 * P), ("ut", 16), ("wt", 512), ("ub", 1280), ("st", 2048
                ("mkt", 4 * P), ("zz", 544), ("wft", 512), ("mt", 512), ("oneb", P), ("er", 256), ("cw", 256), ("rb", 128), ("rk0", P), ("rk1", P)):
     _buf(_n, _c, BF)
 for _n, _c in (("th0", P), ("th1", P), ("thn", P), ("zf", P), ("one32", 32), ("up32", 32), ("eye32", 32), ("mw", 16), ("mwb", 16), ("m8", 8),
-               ("d16", 8), ("dm", 8), ("cf", 16), ("ohb", 16), ("oha", 16), ("ohv", 16), ("pm", 200), ("inp", 8), ("tb", 32), ("hp", 16),
-               ("tt", 32), ("ne", 32), ("mb", 32), ("mr", 32), ("le", 40), ("dg", 32), ("xa", 24), ("hd", 4 * P), ("ha", 128),
-               ("yw", 256), ("yo", P), ("tgb", 16), ("js", 200)):
+               ("nk", 16), ("d0", 64), ("d1", 64), ("ms", 64), ("d16", 8), ("dm", 8), ("cf", 16), ("ohb", 16), ("ohh", 16), ("oha", 16),
+               ("pm", 200), ("tb", 32), ("tt", 32), ("ne", 64), ("dg", 32), ("xa", 24), ("hd", 4 * P), ("ha", 128),
+               ("yw", 256), ("yo", P), ("tgb", 16), ("js0", 16), ("js1", P), ("js2", 200), ("js3", 16), ("js4", 64), ("js5", P)):
     _buf(_n, _c, F32)
 _buf("ic", 16, I32)
 _buf("ol", 2, U16)
@@ -152,7 +154,7 @@ def rank_program(g, core, T, topo):
         elif kind == "pick":
             cost = 0.07 + 0.0016 * _size(writes[0])
         elif q == "T":
-            cost = 0.0015 * (_size(writes[0]) + 16)
+            cost = MMC * (_size(writes[0]) + 16)
         elif q == "G":
             cost = 0.2 + 0.002 * n
         else:
@@ -161,7 +163,7 @@ def rank_program(g, core, T, topo):
         return add(q, reads, writes, cost, cost, call)
 
     def dma(q, out, in_, sem, reads, writes):
-        add(q, reads, writes, 0.1, 2.2, lambda: queue[q].dma_start(out, in_), sem, 16)
+        add(q, reads, writes, 0.1, LOAD, lambda: queue[q].dma_start(out, in_), sem, 16)
 
     def emit():
         count = {"V": 0, "S": 0, "T": 0, "G": 0}
@@ -196,6 +198,9 @@ def rank_program(g, core, T, topo):
 
     V, S = g.vector, g.scalar
 
+    def val(s):
+        return ap(s) if isinstance(s, tuple) else s
+
     def fill(x, v):
         do("V", [], [x], lambda: V.memset(ap(x), v))
 
@@ -204,11 +209,10 @@ def rank_program(g, core, T, topo):
 
     def ts(o, i, s1, s2, op0, op1=None):
         rd = [i] + [s for s in (s1, s2) if isinstance(s, tuple)]
-        a, b = (ap(s) if isinstance(s, tuple) else s for s in (s1, s2))
         if op1 is None:
-            do("V", rd, [o], lambda: V.tensor_scalar(ap(o), ap(i), a, None, op0))
+            do("V", rd, [o], lambda: V.tensor_scalar(ap(o), ap(i), val(s1), None, op0))
         else:
-            do("V", rd, [o], lambda: V.tensor_scalar(ap(o), ap(i), a, b, op0, op1))
+            do("V", rd, [o], lambda: V.tensor_scalar(ap(o), ap(i), val(s1), val(s2), op0, op1))
 
     def tt(o, i0, i1, op):
         do("V", [i0, i1], [o], lambda: V.tensor_tensor(ap(o), ap(i0), ap(i1), op))
@@ -217,18 +221,18 @@ def rank_program(g, core, T, topo):
         do("V", [i], [o], lambda: V.tensor_reduce(ap(o), ap(i), AxisListType.X, op))
 
     def scan(o, d0, d1, init, op0, op1):
-        do("V", [d0, d1], [o], lambda: V.tensor_tensor_scan(ap(o), ap(d0), ap(d1), init, op0, op1))
+        rd = [d0, d1] + ([init] if isinstance(init, tuple) else [])
+        do("V", rd, [o], lambda: V.tensor_tensor_scan(ap(o), ap(d0), ap(d1), val(init), op0, op1))
 
     def turn(o, i):
         do("V", [i], [o], lambda: V.transpose(ap(o), ap(i)))
 
     def act(o, i, f=Act.Identity, bias=0.0, scale=1.0, acc=None):
         rd = [i] + [s for s in (bias, scale) if isinstance(s, tuple)]
-        b, c = (ap(s) if isinstance(s, tuple) else s for s in (bias, scale))
         if acc is None:
-            do("S", rd, [o], lambda: S.activation(ap(o), ap(i), f, bias=b, scale=c))
+            do("S", rd, [o], lambda: S.activation(ap(o), ap(i), f, bias=val(bias), scale=val(scale)))
         else:
-            do("S", rd, [o, acc], lambda: S.activation(ap(o), ap(i), f, bias=b, scale=c, accum_out=ap(acc)))
+            do("S", rd, [o, acc], lambda: S.activation(ap(o), ap(i), f, bias=val(bias), scale=val(scale), accum_out=ap(acc)))
 
     def quant(n, c0, c1, i):
         q, s = A(n + "q", c0, c1), A(n + "s", c0, c1)
@@ -270,11 +274,12 @@ def rank_program(g, core, T, topo):
 
     dma("Y", T.ct[:, :], T.c[:, :], "lc", [], [whole("ct", 4 * P)])
     dma("S", T.ut[:, 0:16], T.u[:, 0:16], "lu", [], [whole("ut", 16)])
-    dma("Y", T.wt[:, :], T.w[:, :], "lw", [], [whole("wt", 512)])
+    dma("Y", T.wt[:, :], T.w[:, :], "lw", [whole("ct", 4 * P)], [whole("wt", 512)])
 
     fill(whole("zz", 544), 0.0)
     fill(whole("thn", P), -TINY)
     fill(whole("oneb", P), 1.0)
+    fill(whole("zf", P), 0.0)
     iota(A("ic", 0, 1), [[0, 1]], 0, 1)
     iota(whole("er", 256), [[0, 8], [1, 16], [16, 2]], 0, 0)
     for h in range(2):
@@ -288,7 +293,6 @@ def rank_program(g, core, T, topo):
     ts(A("ic", 1, 2), A("ic", 0, 1), 112, None, Op.bitwise_and)
     ts(A("ic", 2, 3), A("ic", 0, 1), 15, None, Op.bitwise_and)
     copy(A("cf", 0, 2), A("ic", 1, 3))
-    fill(whole("zf", P), 0.0)
     ts(cf(2), cf(0), 64.0, None, Op.add)
     copy(cf(3), cf(1))
     fill(A("cf", 2, 4, 1, 0, 64), 0.0)
@@ -299,31 +303,32 @@ def rank_program(g, core, T, topo):
     def query(t):
         for b in range(4):
             one = A("ut", 4 * t + b, 4 * t + b + 1)
-            if t == 0:
+            if t == 0 and b < 2:
                 ts(A("ub", 512 + b, 1280, 4), A("oneb", 0, P), one, None, Op.mult)
             else:
                 act(A("ub", 512 + b, 1280, 4), whole("zf", P), bias=one)
-        if t == 0:
-            quant("u0", 128, 320, A("ub", 512, 1280))
         for b in range(4):
             one = A("ut", 4 * t + b, 4 * t + b + 1)
             ts(A("ub", b, 512, 4), A("oneb", 0, 128), one, -1.0, Op.mult, Op.mult)
-        if t == 0:
-            quant("x0", 0, P, whole("ct", 4 * P))
-            quant("u0", 0, 128, A("ub", 0, 512))
-        else:
-            quant("u%d" % t, 0, 320, whole("ub", 1280))
+        quant("u%d" % t, 0, 320, whole("ub", 1280))
 
     query(0)
+    quant("x0", 0, P, whole("ct", 4 * P))
     fill(A("cmt", 2, 4 * P, 4), 0.0)
     fill(A("cmt", 3, 4 * P, 4), 0.0)
     for t in range(R):
         quant("v%d" % t, P + K, P + 160, zero)
     fill(Z("one32", 0, 32), 1.0)
     fill(Z("pm", 0, 1), LOW)
+    fill(Z("ne", 32, 64), 0.0)
+    fill(Z("d0", 0, 32), 1.0)
+    fill(Z("d0", 32, 33), -1.0)
+    fill(Z("d0", 48, 64), 0.0)
+    fill(Z("d1", 32, 48), 0.0)
     iota(whole("cw", 256), [[0, 8], [1, 16], [0, 2]], 1, 0)
-    iota(whole("mw", 12), [[1, 12]], 0, 0)
-    iota(Z("mwb", 0, 12), [[2, 12]], -12, 0)
+    iota(whole("mw", 16), [[1, 16]], 0, 0)
+    iota(Z("nk", 0, 16), [[-1, 16]], 0, 0)
+    iota(whole("mwb", 12), [[2, 12]], -12, 0)
     sel(A("st", 0, 512, 4), A("oneb", 0, 128), [[-1, 128]], Op.is_equal, 0, 1)
     iota(whole("rb", 128), [[0, 8], [1, 4], [0, 4]], 0, 0)
     iota(Z("m8", 0, 8), [[1, 8]], 0, 0)
@@ -339,8 +344,9 @@ def rank_program(g, core, T, topo):
         fill(A("kst", 513, 1024, 4, 64, 128), 1.0)
         copy(A("cf", 4, 8), A("ic", 3, 7))
         ts(cf(10), cf(1), 1.0, None, Op.add)
-        ts(cf(8), cf(5), 0.5, None, Op.add)
         ts(cf(9), cf(7), 224.0, None, Op.add)
+        ts(cf(11), cf(5), -BIG, None, Op.mult)
+        ts(cf(12), cf(5), -1.0, -0.5, Op.mult, Op.add)
         for b in range(2):
             ts(Z("kst", 1536 + b, 2048, 4), Z("rb", 0, 128), cf(4, L), None, Op.is_equal)
         quant("kc", 128, 512, A("kst", 512, 2048))
@@ -352,8 +358,8 @@ def rank_program(g, core, T, topo):
 
     def later():
         ts(Z("d16", 0, 8), Z("m8", 0, 8), cf(6, L), 16.0, Op.is_equal, Op.mult)
-        ts(Z("dm", 0, 8), Z("m8", 0, 8), cf(6, L), -1000.0, Op.not_equal, Op.mult)
-        ts(Z("dm", 0, 8), Z("dm", 0, 8), -0.0625, None, Op.add)
+        ts(Z("dm", 0, 8), Z("m8", 0, 8), cf(6, L), -16000.0, Op.not_equal, Op.mult)
+        ts(Z("dm", 0, 8), Z("dm", 0, 8), -1.0, None, Op.add)
         fill(A("wft", 0, 512, 4, 32, 33), 1.0)
         ts(A("wft", 2, 512, 4, 32, 33), A("cw", 0, 256, 2, 32, 33), -1.0, None, Op.add)
         ts(A("zz", 32, 80, 4, 32, 33), A("mw", 0, 12, 1, 32, 33), 16.0, None, Op.mult)
@@ -365,14 +371,14 @@ def rank_program(g, core, T, topo):
         def sc(k):
             return Z(c, k, k + 1)
         if part == 1:
+            ts(sc(23), sc(1), 1.0, sc(9), Op.subtract, Op.mult)
+            ts(sc(24), sc(5), -0.5, None, Op.mult)
+            ts(sc(25), sc(5), -97.0, sc(23), Op.mult, Op.add)
             tt(Z("dg", 0, 32), Z("cr%d" % t, 0, 32), Z("eye32", 0, 32), Op.mult)
             red(sc(20), Z("dg", 0, 32), Op.add)
-            ts(sc(21), sc(20), -0.5, None, Op.add)
-            act(Z("js", 0, P), Z("gi%d" % t, 0, P), Act.Sign, bias=sc(21), scale=-1.0 / BIG, acc=sc(22))
+            act(Z("js5", 0, P), Z("gi%d" % t, 0, P), Act.Sign, bias=sc(20), scale=-1.0 / BIG, acc=sc(22))
         else:
-            ts(sc(23), sc(22), -0.5, -97.0, Op.mult, Op.add)
-            ts(sc(24), sc(1), sc(23), 1.0, Op.subtract, Op.subtract)
-            ts(Z("tgb", t, t + 1), sc(24), sc(5), sc(23), Op.mult, Op.add)
+            act(Z("tgb", t, t + 1), sc(22), scale=sc(24), bias=sc(25))
             dma("Y", T.tg[t:t + 1, :], T.tgb[0:L, t:t + 1], "tg_%d" % t, [Z("tgb", t, t + 1)], [])
 
     for t in range(R):
@@ -381,6 +387,9 @@ def rank_program(g, core, T, topo):
 
         def sc(k):
             return Z(c, k, k + 1)
+
+        def sca(k):
+            return A(c, k, k + 1)
         pair = []
         for h in range(2):
             pair.append(mm("b%d" % h, (x, 64 * h, 64 * h + 128), (u, 128, 320), True, False))
@@ -409,10 +418,10 @@ def rank_program(g, core, T, topo):
         mask, en = topo.mask(core, dst), len(topo.engines(core, dst))
         to = (T.sem["arr%d" % t], T.sem["sent%d" % t], pid, rid, mask)
         vq, nq, vs, ns = T[v + "q"][:, P:P + K], T[n + "q"][:, 0:K], T[v + "s"][:, P:P + K], T[n + "s"][:, 0:K]
-        m1 = add("G", [A(n + "q", 0, K)], [], 0.9, 0.9, lambda vq=vq, nq=nq, to=to: g.remote_dma(vq.bitcast(dt.uint8), nq.bitcast(dt.uint8), *to), "sent%d" % t, 2 * en)
-        m2 = add("G", [A(n + "s", 0, K)], [], 0.9, 0.9, lambda vs=vs, ns=ns, to=to: g.remote_dma(vs, ns, *to), "sent%d" % t, 2 * en)
+        m1 = add("G", [A(n + "q", 0, K)], [], ISSUE, ISSUE, lambda vq=vq, nq=nq, to=to: g.remote_dma(vq.bitcast(dt.uint8), nq.bitcast(dt.uint8), *to), "sent%d" % t, 2 * en)
+        m2 = add("G", [A(n + "s", 0, K)], [], ISSUE, ISSUE, lambda vs=vs, ns=ns, to=to: g.remote_dma(vs, ns, *to), "sent%d" % t, 2 * en)
         m2["after"][m1["n"]] = False
-        fly = add("arrive", [], [A(v + "q", P, P + K), A(v + "s", P, P + K)], 1.6, 1.6, None, "arr%d" % t, 2 * en)
+        fly = add("arrive", [], [A(v + "q", P, P + K), A(v + "s", P, P + K)], FLIGHT, FLIGHT, None, "arr%d" % t, 2 * en)
         fly["after"].update({m1["n"]: False, m2["n"]: False})
         dma("Y", T[v + "q"][:, 0:P].bitcast(dt.uint8), T[x + "q"][:, 0:P].bitcast(dt.uint8), "cq%d" % t, [A(x + "q", 0, P)], [A(v + "q", 0, P)])
         dma("Y", T[v + "s"][:, 0:P], T[x + "s"][:, 0:P], "cs%d" % t, [A(x + "s", 0, P)], [A(v + "s", 0, P)])
@@ -424,24 +433,29 @@ def rank_program(g, core, T, topo):
         copy(A("mkt", 1, 4 * P, 4), A("mkt", 0, 4 * P, 4))
         act(A("mkt", 2, 4 * P, 4), A("mkt", 0, 4 * P, 4), Act.Copy)
         copy(A("mkt", 3, 4 * P, 4), A("mkt", 0, 4 * P, 4))
-        scan(Z(gi, 0, P), Z("mkt", 0, 4 * P, 4), Z("zf", 0, P), 0.0, Op.add, Op.add)
+        scan(A(gi, 0, P), A("mkt", 0, 4 * P, 4), A("zz", 80, 80 + P), cf(11), Op.add, Op.add)
         quant("mk", 0, P, whole("mkt", 4 * P))
-        act(Z("js", 0, 12), Z(gi, 15, P, 16), Act.Sign, bias=cf(8, L), scale=-1.0 / BIG, acc=sc(10))
-        act(Z("js", 0, P), Z(gi, 0, P), Act.Sign, bias=cf(8, L), scale=-1.0 / BIG, acc=sc(11))
+        act(A("js0", 0, 12), A(gi, 15, P, 16), Act.Sign, bias=0.5, scale=-1.0 / BIG, acc=sca(10))
+        act(A("js1", 0, P), A(gi, 0, P), Act.Sign, bias=0.5, scale=-1.0 / BIG, acc=sca(11))
         if t == 0:
             later()
         for b in range(4):
             bank = ("b6", "b7", "b0", "b1")[b]
             mm(bank, ("eb", 128 * b, 128 * b + 128), (x, 0, P))
             act(A("hd", b, 4 * P, 4), A(bank, 0, P), Act.Copy, scale=0.5)
-        for k in range(4):
+        for k in range(3):
             mm("b5", NEG, ("mk", 0, P), k == 0, False)
-        ts(Z("ohb", 0, 12), Z("mwb", 0, 12), sc(10), None, Op.is_equal)
-        ts(sc(12), sc(10), -8.0, 96.0, Op.mult, Op.add)
-        ts(sc(13), sc(10), -16.0, sc(11), Op.mult, Op.add)
-        ts(sc(14), sc(13), 0.5, 1.0, Op.mult, Op.add)
-        ts(Z("le", 32, 33), sc(13), -0.5, None, Op.mult)
-        ts(Z("wft", 1, 512, 2), Z("cw", 0, 256), sc(14), None, Op.is_equal)
+        ts(A("ohb", 0, 12), A("mwb", 0, 12), sca(10), None, Op.is_equal)
+        ts(Z("ohh", 0, 12), Z("mwb", 0, 12), sc(10), 0.5, Op.is_equal, Op.mult)
+        ts(sc(12), sc(10), -8.0, 112.0, Op.mult, Op.add)
+        ts(sca(13), sca(10), -16.0, sca(11), Op.mult, Op.add)
+        ts(sca(14), sca(13), 0.5, 1.0, Op.mult, Op.add)
+        ts(sc(15), sc(13), -0.5, 16.0, Op.mult, Op.add)
+        ts(sca(16), sca(13), -0.5, None, Op.mult)
+        ts(A("wft", 1, 512, 2), whole("cw", 256), sca(14), None, Op.is_equal)
+        act(A("zz", 35, 80, 4, 64, 96), A("ohb", 0, 12, 1, 64, 96), scale=A(c, 16, 17, 1, 64, 96))
+        ts(Z("d0", 33, 48), Z("mw", 1, 16), sc(15), None, Op.is_lt)
+        ts(Z("d1", 48, 64), Z("nk", 0, 16), sc(15), 0.0, Op.add, Op.max)
         if t == 0:
             quant("w", 0, 128, whole("wt", 512))
         if not last:
@@ -461,42 +475,37 @@ def rank_program(g, core, T, topo):
         scan(Z("pm", 1, 1 + P), A("b5", 0, P, 1, 0, L), Z("zf", 0, P), LOW, Op.max, Op.add)
         top = Z("pm", P, P + 1)
         half(0)
-        ts(Z("hp", 0, 12), Z("pm", 16, 1 + P, 16), top, None, Op.is_lt)
-        red(sc(0), Z("hp", 0, 12), Op.add)
-        act(Z("js", 0, 1 + P), Z("pm", 0, 1 + P), Act.Sign, bias=top, scale=-1.0, acc=sc(1))
-        ts(Z("inp", 0, 8), Z("dm", 0, 8), sc(0), 16.0, Op.subtract, Op.mult)
-        ts(Z("zz", 0, 32, 4), Z("d16", 0, 8), sc(0), None, Op.mult)
-        ts(Z("oha", 0, 12), Z("mw", 0, 12), sc(0), None, Op.is_equal)
-        ts(sc(2), sc(0), -16.0, cf(9, L), Op.mult, Op.add)
+        act(Z("js2", 0, 1 + P), Z("pm", 0, 1 + P), Act.Sign, bias=top, scale=-1.0, acc=sc(1))
+        act(Z("js3", 0, 12), Z("pm", 16, 1 + P, 16), Act.Sign, bias=top, scale=-1.0, acc=sc(0))
         act(Z("tb", 0, 32), Z("up32", 0, 32), scale=sc(1))
         act(sc(3), sc(0), scale=-16.0, bias=sc(1))
+        act(Z("zz", 0, 32, 4), Z("d16", 0, 8), scale=sc(0))
+        ts(Z("oha", 0, 12), Z("mw", 0, 12), sc(0), None, Op.is_equal)
+        act(sc(2), sc(0), scale=-16.0, bias=cf(9, L))
         act(Z("xa", 0, 24, 2), Z("oha", 0, 12), scale=sc(2))
         act(sc(4), sc(3), scale=-1.0, bias=cf(10, L))
         half(1)
         act(Z("xa", 1, 24, 2), Z("oha", 0, 12), scale=sc(4))
         half(2)
         half(3)
-        ts(Z("zz", 1, 32, 4), Z("inp", 0, 8), sc(1), 0.0, Op.add, Op.max)
+        ts(Z("zz", 1, 32, 4), Z("dm", 0, 8), sc(3), 0.0, Op.add, Op.max)
         turn(Z("tt", 0, 32), Z("tb", 0, 32))
         quant("xo", 0, 128, A("zz", 0, 512))
         mm("b3", W1, ("xo", 0, 128))
-        ts(Z("ne", 0, 32), Z("tt", 0, 32), sc(1), None, Op.not_equal)
+        ts(Z("ne", 0, 32), Z("tt", 0, 32), sc(1), None, Op.is_equal)
         ts(Z("wft", 0, 512, 2), Z("cw", 0, 256), sc(3), None, Op.is_equal)
-        red(sc(5), Z("ne", 0, 32), Op.min)
-        act(Z("mb", 0, 32), Z("one32", 0, 32), scale=sc(5))
-        act(Z("zz", 32, 80, 2), Z("xa", 0, 24), scale=sc(5))
+        scan(Z("ms", 0, 64), Z("ne", 0, 64), Z("zf", 0, 64), 0.0, Op.max, Op.max)
+        act(sc(9), Z("ms", 31, 32), scale=-1.0, bias=1.0)
+        act(sc(5), Z("ms", 31, 32))
+        act(Z("zz", 32, 80, 2), Z("xa", 0, 24), scale=sc(9))
         quant("wf", 0, 128, whole("wft", 512))
         ts(A("om", 0, 8), A("b3", 0, 8), 4.0, cf(4), Op.mult, Op.add)
-        turn(Z("mr", 0, 32), Z("mb", 0, 32))
-        scan(Z(cr, 0, 32), Z("one32", 0, 32), Z("mr", 0, 32), 0.0, Op.add, Op.subtract)
-        ts(Z("le", 0, 32), Z(cr, 0, 32), cf(5, L), None, Op.is_le)
-        ts(Z("le", 33, 34), Z(cr, 15, 16), cf(5, L), -16.0, Op.is_le, Op.mult)
-        ts(sc(6), Z(cr, 31, 32), cf(5, L), None, Op.is_gt)
-        red(sc(7), Z("le", 0, 34), Op.add)
-        ts(Z("ohv", 0, 12), Z("ohb", 0, 12), sc(6), None, Op.mult)
-        act(sc(8), Z("le", 33, 34), scale=-1.0, bias=sc(12))
-        act(Z("zz", 33, 80, 4), Z("ohv", 0, 12), scale=sc(8))
-        ts(Z("zz", 35, 80, 4), Z("ohb", 0, 12), sc(7), sc(6), Op.mult, Op.mult)
+        turn(Z("d1", 0, 32), Z("ms", 32, 64))
+        scan(Z(cr, 0, 64), Z("d0", 0, 64), Z("d1", 0, 64), cf(12, L), Op.mult, Op.add)
+        act(Z("js4", 0, 64), Z(cr, 0, 64), Act.Sign, scale=-1.0, acc=sc(7))
+        ts(sc(6), Z(cr, 31, 32), 0.0, sc(12), Op.is_gt, Op.mult)
+        ts(Z("zz", 33, 80, 4), Z("ohb", 0, 12), sc(6), None, Op.mult)
+        act(Z("zz", 35, 80, 4), Z("ohh", 0, 12), scale=sc(7))
         quant("xf", 0, 128, A("zz", 32, 544))
         mm("b2", ("wf", 0, 128), ("xf", 0, 128))
         ho, hi_, of, ha = A("mt", 0, 128), A("hd", 0, 4 * P), A("om", 0, 8), A("ha", 0, 128)
@@ -510,13 +519,15 @@ def rank_program(g, core, T, topo):
         else:
             mm("b3", ("w", 0, 128), (v, P, P + 128))
             act(A("yw", P, P + 64), A("b3", 0, 64), Act.Copy)
-            pick_codes(A(nx + "q", 0, P), A(v + "q", 0, 256), A("of", 0, 12))
+            for a, b in ((0, 6), (6, 12)):
+                pick_codes(A(nx + "q", 16 * a, 16 * b), A(v + "q", 0, 256), A("of", a, b))
             pick_s(A("yo", 0, P), A("yw", 0, 256), A("of", 0, 12))
             dma("Y", T.oc[:, :], T.x3q[:, 0:P].bitcast(dt.uint8), "oc_", [A("x3q", 0, P)], [])
             dma("S", T.y[:, :], T.yo[:, 0:P], "oy_", [A("yo", 0, P)], [])
-            place(t, 1)
-            pick_v(A(nx + "s", 0, P), A(v + "s", 0, 256), A("of", 0, 12))
+            pick_v(A(nx + "s", 0, 96), A(v + "s", 0, 256), A("of", 0, 6))
+            pick_s(A(nx + "s", 96, P), A(v + "s", 0, 256), A("of", 6, 12))
             for k in range(4):
                 dma("Y", T.osc[4 * k:4 * k + 4, :], T.x3s[32 * k:32 * k + 4, 0:P], "os%d" % k, [A("x3s", 0, P)], [])
+            place(t, 1)
             place(t, 2)
     emit()

from concourse.mybir import dt, AluOpType as Op, AxisListType, ActivationFunctionType as Act

N, P, K, R = 8, 192, 32, 3
TINY = 1e-30
BIG = 2.0 ** 30
LOW = -1e29
WAKE, SLACK = 0.18, 0.3
LOAD, ISSUE, FLIGHT = 1.1, 0.4, 1.0
MMC = 0.0012

MXC, U8, F32, BF, I32, U16 = "float8_e4m3fn_x4", "uint8", "float32", "bfloat16", "int32", "uint16"
SCRATCH = {}


def _buf(name, cols, dtype, where="sbuf"):
    SCRATCH[name] = (where, [128, cols], dtype)


def _pair(name, cols):
    _buf(name + "q", cols, MXC)
    _buf(name + "s", cols, U8)


for _t in range(R):
    _pair("x%d" % _t, P)
    _pair("v%d" % _t, P + 160)
    _pair("n%d" % _t, K)
    _pair("u%d" % _t, 320)
    _buf("sc%d" % _t, 32, F32)
    _buf("cr%d" % _t, 64, F32)
    _buf("gi%d" % _t, P, BF)
_pair("x3", P)
for _n, _c in (("w", 128), ("eb", 512), ("kc", 512), ("e", 128), ("cm", P), ("mk", P), ("xo", 128), ("wf", 128), ("xf", 128)):
    _pair(_n, _c)
for _n, _c in (("ct", 4 * P), ("ut", 16), ("wt", 512), ("ub", 1280), ("st", 2048), ("kst", 2048), ("et", 512), ("cmt", 4 * P),
               ("mkt", 4 * P), ("zz", 544), ("wft", 512), ("mt", 512), ("oneb", P), ("er", 256), ("cw", 256), ("rb", 128), ("rk0", P), ("rk1", P)):
    _buf(_n, _c, BF)
for _n, _c in (("th0", P), ("th1", P), ("thn", P), ("zf", P), ("one32", 32), ("up32", 32), ("eye32", 32), ("mw", 16), ("mwb", 16), ("m8", 8),
               ("nk", 16), ("d0", 64), ("d1", 64), ("ms", 64), ("d16", 8), ("dm", 8), ("cf", 16), ("ohb", 16), ("ohh", 16), ("oha", 16),
               ("pm", 200), ("tb", 32), ("tt", 32), ("ne", 64), ("dg", 32), ("xa", 24), ("hd", 4 * P), ("ha", 128),
               ("yw", 256), ("yo", P), ("tgb", 16), ("js0", 16), ("js1", P), ("js2", 200), ("js3", 16), ("js4", 64), ("js5", P)):
    _buf(_n, _c, F32)
_buf("ic", 16, I32)
_buf("ol", 2, U16)
_buf("om", 8, U16)
_buf("of", 12, U16)
for _n in range(8):
    _buf("b%d" % _n, 512, F32, "psum")

SEMAPHORES = ["sv", "ss", "stn", "sg", "lc", "lu", "lw", "oc_", "oy_"] + ["os%d" % k for k in range(4)] + ["tg_%d" % k for k in range(R)] \
    + ["arr%d" % k for k in range(R)] + ["sent%d" % k for k in range(R)] + ["cq%d" % k for k in range(R)] + ["cs%d" % k for k in range(R)]


def _cross(a, b):
    if a[1] >= b[2] or b[1] >= a[2] or a[3] >= b[4] or b[3] >= a[4]:
        return False
    m = min(a[5], b[5])
    if m > 1 and a[5] % m == 0 and b[5] % m == 0:
        return (a[3] - b[3]) % m == 0
    return True


def _within(a, b):
    if not (a[1] <= b[1] and b[2] <= a[2] and a[3] <= b[3] and b[4] <= a[4]):
        return False
    return a[5] == 1 or (a[5] == b[5] and (a[3] - b[3]) % a[5] == 0)


def _size(x):
    return (x[4] - x[3] + x[5] - 1) // x[5]


def _order(nodes):
    users = [[] for m in nodes]
    for m in nodes:
        for d in m["after"]:
            users[d].append(m["n"])
    way = [0.0] * len(nodes)
    for m in reversed(nodes):
        way[m["n"]] = max([m["late"]] + [m["late"] + WAKE * nodes[k]["after"][m["n"]] + way[k] for k in users[m["n"]]])
    left = [len(m["after"]) for m in nodes]
    ready = [0.0] * len(nodes)
    free = {}
    able = [m["n"] for m in nodes if not m["after"]]
    done = []
    while able:
        best = None
        for q in set(nodes[k]["q"] for k in able):
            ks = [k for k in able if nodes[k]["q"] == q]
            t0 = max(free.get(q, 0.0), min(ready[k] for k in ks))
            ks = [k for k in ks if ready[k] <= t0 + SLACK]
            k = max(ks, key=lambda i: (way[i], -i))
            now = [i for i in ks if ready[i] <= t0 and t0 + 1.8 * nodes[i]["busy"] <= ready[k] + 0.02]
            if ready[k] > t0 and now:
                k = max(now, key=lambda i: (way[i], -i))
            t = max(t0, ready[k])
            if best is None or (t, q) < best[:2]:
                best = (t, q, k)
        t, q, k = best
        able.remove(k)
        free[q] = t + nodes[k]["busy"]
        done.append(k)
        for i in users[k]:
            ready[i] = max(ready[i], t + nodes[k]["late"] + (WAKE if nodes[i]["after"][k] else 0.0))
            left[i] -= 1
            if not left[i]:
                able.append(i)
    return done


def rank_program(g, core, T, topo):
    rank = T.rank_of(core)
    if rank is None:
        return
    queue = {"V": g.vector, "S": g.scalar, "T": g.tensor, "G": g, "Y": g.sync}
    own = {"V": "sv", "S": "ss", "T": "stn", "G": "sg"}
    log = {}
    nodes = []

    def A(name, c0, c1, step=1, p0=0, p1=128):
        return (name, p0, p1, c0, c1, step)

    def ap(x):
        return T[x[0]][x[1]:x[2], x[3]:x[4]:x[5]] if x[5] > 1 else T[x[0]][x[1]:x[2], x[3]:x[4]]

    def psum(x):
        return SCRATCH[x[0]][0] == "psum"

    def add(q, reads, writes, busy, late, issue, sem=None, val=0):
        after = {}
        node = {"q": q, "n": len(nodes), "after": after, "busy": busy, "late": late, "issue": issue, "sem": sem, "val": val}
        for views, w in ((reads, False), (writes, True)):
            for x in views:
                for y, m, yw in log.get(x[0], []):
                    if psum(x):
                        if q == "T" and m["q"] == "T":
                            after.setdefault(m["n"], False)
                        elif q != m["q"] or w or yw:
                            after[m["n"]] = True
                    elif (w or yw) and _cross(x, y):
                        after[m["n"]] = True
        for x in writes:
            log[x[0]] = [e for e in log.get(x[0], []) if not _within(x, e[0]) or (psum(x) and q == "T" and e[1]["q"] == "T")]
        for views, w in ((reads, False), (writes, True)):
            for x in views:
                log.setdefault(x[0], []).append((x, node, w))
        nodes.append(node)
        return node

    def do(q, reads, writes, call, kind=""):
        n = max(_size(x) for x in reads[:1] + writes[:1])
        if kind == "quant":
            cost = 0.015 + 0.000275 * _size(reads[0])
        elif kind == "pick":
            cost = 0.07 + 0.0016 * _size(writes[0])
        elif q == "T":
            cost = MMC * (_size(writes[0]) + 16)
        elif q == "G":
            cost = 0.2 + 0.002 * n
        else:
            two = q == "V" and all(SCRATCH[x[0]][2] in (BF, U16) for x in reads[:1] + writes[:1])
            cost = max(64, n * (0.5 if two else 1)) * 0.00104
        return add(q, reads, writes, cost, cost, call)

    def dma(q, out, in_, sem, reads, writes):
        add(q, reads, writes, 0.1, LOAD, lambda: queue[q].dma_start(out, in_), sem, 16)

    def emit():
        count = {"V": 0, "S": 0, "T": 0, "G": 0}
        known = {q: {} for q in queue}
        every = {}
        done = _order(nodes)
        at = {k: i for i, k in enumerate(done)}
        for k in done:
            m = nodes[k]
            q = m["q"]
            if q in queue:
                for d in sorted(m["after"], reverse=True, key=lambda i: at[i]):
                    o = nodes[d]
                    if not m["after"][d] or known[q].get(o["sem"], 0) >= o["val"]:
                        continue
                    queue[q].wait_ge(T.sem[o["sem"]], o["val"])
                    for s, v in list(o["clock"].items()) + [(o["sem"], o["val"])]:
                        known[q][s] = max(known[q].get(s, 0), v)
            if m["sem"] is None:
                count[q] += 1
                m["sem"], m["val"] = own[q], count[q]
                m["issue"]().then_inc(T.sem[own[q]], 1)
            elif m["issue"] is not None:
                ins = m["issue"]()
                if m["sem"][0:4] != "sent":
                    ins.then_inc(T.sem[m["sem"]], 16)
            m["clock"] = dict(known.get(q, {}))
            every[m["sem"]] = max(m["val"], every.get(m["sem"], 0))
        final = ["sg", "stn", "ss", "sv"] + ["os%d" % k for k in range(4)] + ["tg_%d" % (R - 1), "oc_", "oy_"]
        for s in [e for e in every if e not in final] + final:
            g.wait_ge(T.sem[s], every[s])

    V, S = g.vector, g.scalar

    def val(s):
        return ap(s) if isinstance(s, tuple) else s

    def fill(x, v):
        do("V", [], [x], lambda: V.memset(ap(x), v))

    def copy(o, i):
        do("V", [i], [o], lambda: V.tensor_copy(ap(o), ap(i)))

    def ts(o, i, s1, s2, op0, op1=None):
        rd = [i] + [s for s in (s1, s2) if isinstance(s, tuple)]
        if op1 is None:
            do("V", rd, [o], lambda: V.tensor_scalar(ap(o), ap(i), val(s1), None, op0))
        else:
            do("V", rd, [o], lambda: V.tensor_scalar(ap(o), ap(i), val(s1), val(s2), op0, op1))

    def tt(o, i0, i1, op):
        do("V", [i0, i1], [o], lambda: V.tensor_tensor(ap(o), ap(i0), ap(i1), op))

    def red(o, i, op):
        do("V", [i], [o], lambda: V.tensor_reduce(ap(o), ap(i), AxisListType.X, op))

    def scan(o, d0, d1, init, op0, op1):
        rd = [d0, d1] + ([init] if isinstance(init, tuple) else [])
        do("V", rd, [o], lambda: V.tensor_tensor_scan(ap(o), ap(d0), ap(d1), val(init), op0, op1))

    def turn(o, i):
        do("V", [i], [o], lambda: V.transpose(ap(o), ap(i)))

    def act(o, i, f=Act.Identity, bias=0.0, scale=1.0, acc=None):
        rd = [i] + [s for s in (bias, scale) if isinstance(s, tuple)]
        if acc is None:
            do("S", rd, [o], lambda: S.activation(ap(o), ap(i), f, bias=val(bias), scale=val(scale)))
        else:
            do("S", rd, [o, acc], lambda: S.activation(ap(o), ap(i), f, bias=val(bias), scale=val(scale), accum_out=ap(acc)))

    def quant(n, c0, c1, i):
        q, s = A(n + "q", c0, c1), A(n + "s", c0, c1)
        do("V", [i], [q, s], lambda: V.quantize_mx(ap(q), ap(s), ap(i)), "quant")

    def mm(o, l, r, start=True, stop=True):
        lq, ls, rq, rs = A(l[0] + "q", l[1], l[2]), A(l[0] + "s", l[1], l[2]), A(r[0] + "q", r[1], r[2]), A(r[0] + "s", r[1], r[2])
        x = A(o, 0, r[2] - r[1])
        return do("T", [lq, ls, rq, rs], [x], lambda: g.tensor.matmul_mx(ap(x), ap(lq), ap(ls), ap(rq), ap(rs), start, stop))

    def pick_codes(o, i, off):
        do("V", [i, off], [o], lambda: V.tensor_copy(ap(o).bitcast(dt.uint32), ap(i).bitcast(dt.uint32).indirect(ap(off))), "pick")

    def pick_s(o, i, off):
        do("S", [i, off], [o], lambda: S.activation(ap(o), ap(i).indirect(ap(off)), Act.Copy), "pick")

    def pick_v(o, i, off):
        do("V", [i, off], [o], lambda: V.tensor_copy(ap(o), ap(i).indirect(ap(off))), "pick")

    def iota(o, pattern, base, cm):
        if SCRATCH[o[0]][2] != I32:
            do("G", [], [o], lambda: g.iota(ap(o), pattern, base, cm, allow_small_or_imprecise_dtypes=True))
        else:
            do("G", [], [o], lambda: g.iota(ap(o), pattern, base, cm))

    def sel(o, i, pattern, op, base, cm):
        do("G", [i], [o], lambda: g.affine_select(ap(o), ap(i), pattern, op, 0.0, base, cm))

    L = 32

    def whole(n, c):
        return A(n, 0, c)

    def Z(n, c0, c1, step=1):
        return A(n, c0, c1, step, 0, L)

    def cf(k, p1=128):
        return A("cf", k, k + 1, 1, 0, p1)

    dma("Y", T.ct[:, :], T.c[:, :], "lc", [], [whole("ct", 4 * P)])
    dma("S", T.ut[:, 0:16], T.u[:, 0:16], "lu", [], [whole("ut", 16)])
    dma("Y", T.wt[:, :], T.w[:, :], "lw", [whole("ct", 4 * P)], [whole("wt", 512)])

    fill(whole("zz", 544), 0.0)
    fill(whole("thn", P), -TINY)
    fill(whole("oneb", P), 1.0)
    fill(whole("zf", P), 0.0)
    iota(A("ic", 0, 1), [[0, 1]], 0, 1)
    iota(whole("er", 256), [[0, 8], [1, 16], [16, 2]], 0, 0)
    for h in range(2):
        sel(whole("th%d" % h, P), whole("thn", P), [[-1, P]], Op.is_gt, 64 * h, 1)
    zero = whole("zz", 512)
    for x in (A("kst", 0, 512), A("st", 0, 512), A("kst", 512, 1024), A("kst", 1536, 2048)):
        act(x, zero, Act.Copy)
    act(A("kst", 1024, 1536), zero, bias=-BIG)
    for x in (whole("wft", 512), whole("mt", 512)):
        act(x, zero, Act.Copy)
    ts(A("ic", 1, 2), A("ic", 0, 1), 112, None, Op.bitwise_and)
    ts(A("ic", 2, 3), A("ic", 0, 1), 15, None, Op.bitwise_and)
    copy(A("cf", 0, 2), A("ic", 1, 3))
    ts(cf(2), cf(0), 64.0, None, Op.add)
    copy(cf(3), cf(1))
    fill(A("cf", 2, 4, 1, 0, 64), 0.0)
    for e, k in ((0, 0), (6, 0), (8, 1), (14, 1)):
        copy(A("kst", e, e + 2), A("cf", k, 4, 2))
    quant("kc", 0, 128, A("kst", 0, 512))

    def query(t):
        for b in range(4):
            one = A("ut", 4 * t + b, 4 * t + b + 1)
            if t == 0 and b < 2:
                ts(A("ub", 512 + b, 1280, 4), A("oneb", 0, P), one, None, Op.mult)
            else:
                act(A("ub", 512 + b, 1280, 4), whole("zf", P), bias=one)
        for b in range(4):
            one = A("ut", 4 * t + b, 4 * t + b + 1)
            ts(A("ub", b, 512, 4), A("oneb", 0, 128), one, -1.0, Op.mult, Op.mult)
        quant("u%d" % t, 0, 320, whole("ub", 1280))

    query(0)
    quant("x0", 0, P, whole("ct", 4 * P))
    fill(A("cmt", 2, 4 * P, 4), 0.0)
    fill(A("cmt", 3, 4 * P, 4), 0.0)
    for t in range(R):
        quant("v%d" % t, P + K, P + 160, zero)
    fill(Z("one32", 0, 32), 1.0)
    fill(Z("pm", 0, 1), LOW)
    fill(Z("ne", 32, 64), 0.0)
    fill(Z("d0", 0, 32), 1.0)
    fill(Z("d0", 32, 33), -1.0)
    fill(Z("d0", 48, 64), 0.0)
    fill(Z("d1", 32, 48), 0.0)
    iota(whole("cw", 256), [[0, 8], [1, 16], [0, 2]], 1, 0)
    iota(whole("mw", 16), [[1, 16]], 0, 0)
    iota(Z("nk", 0, 16), [[-1, 16]], 0, 0)
    iota(whole("mwb", 12), [[2, 12]], -12, 0)
    sel(A("st", 0, 512, 4), A("oneb", 0, 128), [[-1, 128]], Op.is_equal, 0, 1)
    iota(whole("rb", 128), [[0, 8], [1, 4], [0, 4]], 0, 0)
    iota(Z("m8", 0, 8), [[1, 8]], 0, 0)
    sel(Z("up32", 0, 32), Z("one32", 0, 32), [[1, 32]], Op.is_gt, 0, -1)
    sel(Z("eye32", 0, 32), Z("one32", 0, 32), [[1, 32]], Op.is_equal, 0, -1)
    JT, ONES, NEG, W1 = ("kc", 0, 128), ("kc", 128, 256), ("kc", 256, 384), ("kc", 384, 512)

    def columns():
        for k, m in ((3, 3), (4, 31), (6, 16)):
            ts(A("ic", k, k + 1), A("ic", 0, 1), m, None, Op.bitwise_and)
        ts(A("ic", 5, 6), A("ic", 4, 5), 2, None, Op.arith_shift_right)
        fill(A("kst", 512, 1024, 4), 1.0)
        fill(A("kst", 513, 1024, 4, 64, 128), 1.0)
        copy(A("cf", 4, 8), A("ic", 3, 7))
        ts(cf(10), cf(1), 1.0, None, Op.add)
        ts(cf(9), cf(7), 224.0, None, Op.add)
        ts(cf(11), cf(5), -BIG, None, Op.mult)
        ts(cf(12), cf(5), -1.0, -0.5, Op.mult, Op.add)
        for b in range(2):
            ts(Z("kst", 1536 + b, 2048, 4), Z("rb", 0, 128), cf(4, L), None, Op.is_equal)
        quant("kc", 128, 512, A("kst", 512, 2048))

    def decoders():
        for b in range(1, 4):
            act(A("st", 512 * b + b, 512 * b + 512, 4), A("st", 0, 512, 4), Act.Copy)
        quant("eb", 0, 512, whole("st", 2048))

    def later():
        ts(Z("d16", 0, 8), Z("m8", 0, 8), cf(6, L), 16.0, Op.is_equal, Op.mult)
        ts(Z("dm", 0, 8), Z("m8", 0, 8), cf(6, L), -16000.0, Op.not_equal, Op.mult)
        ts(Z("dm", 0, 8), Z("dm", 0, 8), -1.0, None, Op.add)
        fill(A("wft", 0, 512, 4, 32, 33), 1.0)
        ts(A("wft", 2, 512, 4, 32, 33), A("cw", 0, 256, 2, 32, 33), -1.0, None, Op.add)
        ts(A("zz", 32, 80, 4, 32, 33), A("mw", 0, 12, 1, 32, 33), 16.0, None, Op.mult)
        fill(A("zz", 34, 80, 4, 32, 33), 1.0)

    def place(t, part):
        c = "sc%d" % t

        def sc(k):
            return Z(c, k, k + 1)
        if part == 1:
            ts(sc(23), sc(1), 1.0, sc(9), Op.subtract, Op.mult)
            ts(sc(24), sc(5), -0.5, None, Op.mult)
            ts(sc(25), sc(5), -97.0, sc(23), Op.mult, Op.add)
            tt(Z("dg", 0, 32), Z("cr%d" % t, 0, 32), Z("eye32", 0, 32), Op.mult)
            red(sc(20), Z("dg", 0, 32), Op.add)
            act(Z("js5", 0, P), Z("gi%d" % t, 0, P), Act.Sign, bias=sc(20), scale=-1.0 / BIG, acc=sc(22))
        else:
            act(Z("tgb", t, t + 1), sc(22), scale=sc(24), bias=sc(25))
            dma("Y", T.tg[t:t + 1, :], T.tgb[0:L, t:t + 1], "tg_%d" % t, [Z("tgb", t, t + 1)], [])

    for t in range(R):
        x, v, n, u, nx, c, cr, gi = "x%d" % t, "v%d" % t, "n%d" % t, "u%d" % t, "x%d" % (t + 1), "sc%d" % t, "cr%d" % t, "gi%d" % t
        last = t == R - 1

        def sc(k):
            return Z(c, k, k + 1)

        def sca(k):
            return A(c, k, k + 1)
        pair = []
        for h in range(2):
            pair.append(mm("b%d" % h, (x, 64 * h, 64 * h + 128), (u, 128, 320), True, False))
            pair.append(mm("b%d" % h, (u, 0, 128), (x, 0, P), False, True))
        pair[2]["after"].setdefault(pair[1]["n"], False)
        if t > 0:
            place(t - 1, 1)
        tt(A("cmt", 0, 4 * P, 4), A("b0", 0, P), whole("th0", P), Op.is_gt)
        if t == 0:
            for b in (1, 2, 3):
                act(A("st", 512 * b, 512 * b + 512), A("kst", 0, 512), Act.Copy, scale=0.0)
        for h in range(2):
            if h == 1:
                tt(A("cmt", 1, 4 * P, 4), A("b1", 0, P), whole("th1", P), Op.is_gt)
            scan(A("rk%d" % h, 0, P), A("cmt", h, 4 * P, 4), A("zz", 80, 80 + P), 0.0, Op.add, Op.add)
            ts(A("et", h, 512, 2), whole("er", 256), A("rk%d" % h, P - 1, P), None, Op.is_equal)
        quant("e", 0, 128, whole("et", 512))
        mm("b2", ("e", 0, 128), JT)
        quant("cm", 0, P, whole("cmt", 4 * P))
        for m in range(2):
            ts(A("ol", m, m + 1), A("b2", m, m + 1), A("b2", m + 2, m + 3), None, Op.add)
        pick_codes(A(n + "q", 0, K), A(x + "q", 0, P), A("ol", 0, 2))
        pick_s(A(n + "s", 0, K), A(x + "s", 0, P), A("ol", 0, 2))
        dst = T.cores[rank ^ (1 << t)]
        rid, pid = topo.addr(dst, core)
        mask, en = topo.mask(core, dst), len(topo.engines(core, dst))
        to = (T.sem["arr%d" % t], T.sem["sent%d" % t], pid, rid, mask)
        vq, nq, vs, ns = T[v + "q"][:, P:P + K], T[n + "q"][:, 0:K], T[v + "s"][:, P:P + K], T[n + "s"][:, 0:K]
        m1 = add("G", [A(n + "q", 0, K)], [], ISSUE, ISSUE, lambda vq=vq, nq=nq, to=to: g.remote_dma(vq.bitcast(dt.uint8), nq.bitcast(dt.uint8), *to), "sent%d" % t, 2 * en)
        m2 = add("G", [A(n + "s", 0, K)], [], ISSUE, ISSUE, lambda vs=vs, ns=ns, to=to: g.remote_dma(vs, ns, *to), "sent%d" % t, 2 * en)
        m2["after"][m1["n"]] = False
        fly = add("arrive", [], [A(v + "q", P, P + K), A(v + "s", P, P + K)], FLIGHT, FLIGHT, None, "arr%d" % t, 2 * en)
        fly["after"].update({m1["n"]: False, m2["n"]: False})
        dma("Y", T[v + "q"][:, 0:P].bitcast(dt.uint8), T[x + "q"][:, 0:P].bitcast(dt.uint8), "cq%d" % t, [A(x + "q", 0, P)], [A(v + "q", 0, P)])
        dma("Y", T[v + "s"][:, 0:P], T[x + "s"][:, 0:P], "cs%d" % t, [A(x + "s", 0, P)], [A(v + "s", 0, P)])
        if t == 0:
            columns()
            decoders()
        mm("b4", ONES, ("cm", 0, P))
        ts(A("mkt", 0, 4 * P, 4), A("b4", 0, P), 159.5, BIG, Op.is_gt, Op.mult)
        copy(A("mkt", 1, 4 * P, 4), A("mkt", 0, 4 * P, 4))
        act(A("mkt", 2, 4 * P, 4), A("mkt", 0, 4 * P, 4), Act.Copy)
        copy(A("mkt", 3, 4 * P, 4), A("mkt", 0, 4 * P, 4))
        scan(A(gi, 0, P), A("mkt", 0, 4 * P, 4), A("zz", 80, 80 + P), cf(11), Op.add, Op.add)
        quant("mk", 0, P, whole("mkt", 4 * P))
        act(A("js0", 0, 12), A(gi, 15, P, 16), Act.Sign, bias=0.5, scale=-1.0 / BIG, acc=sca(10))
        act(A("js1", 0, P), A(gi, 0, P), Act.Sign, bias=0.5, scale=-1.0 / BIG, acc=sca(11))
        if t == 0:
            later()
        for b in range(4):
            bank = ("b6", "b7", "b0", "b1")[b]
            mm(bank, ("eb", 128 * b, 128 * b + 128), (x, 0, P))
            act(A("hd", b, 4 * P, 4), A(bank, 0, P), Act.Copy, scale=0.5)
        for k in range(3):
            mm("b5", NEG, ("mk", 0, P), k == 0, False)
        ts(A("ohb", 0, 12), A("mwb", 0, 12), sca(10), None, Op.is_equal)
        ts(Z("ohh", 0, 12), Z("mwb", 0, 12), sc(10), 0.5, Op.is_equal, Op.mult)
        ts(sc(12), sc(10), -8.0, 112.0, Op.mult, Op.add)
        ts(sca(13), sca(10), -16.0, sca(11), Op.mult, Op.add)
        ts(sca(14), sca(13), 0.5, 1.0, Op.mult, Op.add)
        ts(sc(15), sc(13), -0.5, 16.0, Op.mult, Op.add)
        ts(sca(16), sca(13), -0.5, None, Op.mult)
        ts(A("wft", 1, 512, 2), whole("cw", 256), sca(14), None, Op.is_equal)
        act(A("zz", 35, 80, 4, 64, 96), A("ohb", 0, 12, 1, 64, 96), scale=A(c, 16, 17, 1, 64, 96))
        ts(Z("d0", 33, 48), Z("mw", 1, 16), sc(15), None, Op.is_lt)
        ts(Z("d1", 48, 64), Z("nk", 0, 16), sc(15), 0.0, Op.add, Op.max)
        if t == 0:
            quant("w", 0, 128, whole("wt", 512))
        if not last:
            query(t + 1)
        else:
            mm("b2", ("w", 0, 128), (x, 0, P))
            act(A("yw", 0, P), A("b2", 0, P), Act.Copy)
        if t > 0:
            place(t - 1, 2)

        mm("b5", (v, P, P + 128), (x, 0, P), False, True)
        for b in range(4):
            mm(("b6", "b7", "b4", "b1")[b], ("eb", 128 * b, 128 * b + 128), (v, P, P + 128))

        def half(b):
            act(A("ha", b, 128, 4), A(("b6", "b7", "b4", "b1")[b], 0, K), Act.Copy, scale=0.5)
        scan(Z("pm", 1, 1 + P), A("b5", 0, P, 1, 0, L), Z("zf", 0, P), LOW, Op.max, Op.add)
        top = Z("pm", P, P + 1)
        half(0)
        act(Z("js2", 0, 1 + P), Z("pm", 0, 1 + P), Act.Sign, bias=top, scale=-1.0, acc=sc(1))
        act(Z("js3", 0, 12), Z("pm", 16, 1 + P, 16), Act.Sign, bias=top, scale=-1.0, acc=sc(0))
        act(Z("tb", 0, 32), Z("up32", 0, 32), scale=sc(1))
        act(sc(3), sc(0), scale=-16.0, bias=sc(1))
        act(Z("zz", 0, 32, 4), Z("d16", 0, 8), scale=sc(0))
        ts(Z("oha", 0, 12), Z("mw", 0, 12), sc(0), None, Op.is_equal)
        act(sc(2), sc(0), scale=-16.0, bias=cf(9, L))
        act(Z("xa", 0, 24, 2), Z("oha", 0, 12), scale=sc(2))
        act(sc(4), sc(3), scale=-1.0, bias=cf(10, L))
        half(1)
        act(Z("xa", 1, 24, 2), Z("oha", 0, 12), scale=sc(4))
        half(2)
        half(3)
        ts(Z("zz", 1, 32, 4), Z("dm", 0, 8), sc(3), 0.0, Op.add, Op.max)
        turn(Z("tt", 0, 32), Z("tb", 0, 32))
        quant("xo", 0, 128, A("zz", 0, 512))
        mm("b3", W1, ("xo", 0, 128))
        ts(Z("ne", 0, 32), Z("tt", 0, 32), sc(1), None, Op.is_equal)
        ts(Z("wft", 0, 512, 2), Z("cw", 0, 256), sc(3), None, Op.is_equal)
        scan(Z("ms", 0, 64), Z("ne", 0, 64), Z("zf", 0, 64), 0.0, Op.max, Op.max)
        act(sc(9), Z("ms", 31, 32), scale=-1.0, bias=1.0)
        act(sc(5), Z("ms", 31, 32))
        act(Z("zz", 32, 80, 2), Z("xa", 0, 24), scale=sc(9))
        quant("wf", 0, 128, whole("wft", 512))
        ts(A("om", 0, 8), A("b3", 0, 8), 4.0, cf(4), Op.mult, Op.add)
        turn(Z("d1", 0, 32), Z("ms", 32, 64))
        scan(Z(cr, 0, 64), Z("d0", 0, 64), Z("d1", 0, 64), cf(12, L), Op.mult, Op.add)
        act(Z("js4", 0, 64), Z(cr, 0, 64), Act.Sign, scale=-1.0, acc=sc(7))
        ts(sc(6), Z(cr, 31, 32), 0.0, sc(12), Op.is_gt, Op.mult)
        ts(Z("zz", 33, 80, 4), Z("ohb", 0, 12), sc(6), None, Op.mult)
        act(Z("zz", 35, 80, 4), Z("ohh", 0, 12), scale=sc(7))
        quant("xf", 0, 128, A("zz", 32, 544))
        mm("b2", ("wf", 0, 128), ("xf", 0, 128))
        ho, hi_, of, ha = A("mt", 0, 128), A("hd", 0, 4 * P), A("om", 0, 8), A("ha", 0, 128)
        do("V", [hi_, of, ha], [ho], lambda: V.tensor_tensor(ap(ho), ap(hi_).indirect(ap(of)), ap(ha), Op.add), "pick")
        quant(v, P + K, P + 160, whole("mt", 512))
        copy(A("of", 0, 12), A("b2", 0, 12))
        if not last:
            for a, b in ((0, 8), (8, 12)):
                pick_codes(A(nx + "q", 16 * a, 16 * b), A(v + "q", 0, 256), A("of", a, b))
                pick_s(A(nx + "s", 16 * a, 16 * b), A(v + "s", 0, 256), A("of", a, b))
        else:
            mm("b3", ("w", 0, 128), (v, P, P + 128))
            act(A("yw", P, P + 64), A("b3", 0, 64), Act.Copy)
            for a, b in ((0, 6), (6, 12)):
                pick_codes(A(nx + "q", 16 * a, 16 * b), A(v + "q", 0, 256), A("of", a, b))
            pick_s(A("yo", 0, P), A("yw", 0, 256), A("of", 0, 12))
            dma("Y", T.oc[:, :], T.x3q[:, 0:P].bitcast(dt.uint8), "oc_", [A("x3q", 0, P)], [])
            dma("S", T.y[:, :], T.yo[:, 0:P], "oy_", [A("yo", 0, P)], [])
            pick_v(A(nx + "s", 0, 96), A(v + "s", 0, 256), A("of", 0, 6))
            pick_s(A(nx + "s", 96, P), A(v + "s", 0, 256), A("of", 6, 12))
            for k in range(4):
                dma("Y", T.osc[4 * k:4 * k + 4, :], T.x3s[32 * k:32 * k + 4, 0:P], "os%d" % k, [A("x3s", 0, P)], [])
            place(t, 1)
            place(t, 2)
    emit()
